import numpy as np
import ml_dtypes


def mxq(x, axis, fmt="e4m3"):
    dtype, down = {"e4m3": (ml_dtypes.float8_e4m3fn, 7), "e5m2": (ml_dtypes.float8_e5m2, 14)}[fmt]
    v = np.moveaxis(np.asarray(x, np.float32).astype(ml_dtypes.bfloat16).astype(np.float64), axis, -1)
    blocks = v.reshape(v.shape[:-1] + (-1, 32))
    amax = np.abs(blocks).max(-1, keepdims=True)
    byte = np.maximum(np.where(amax > 0, np.frexp(amax)[1] - 1 + 127, 0) - down, 1)
    scale = np.exp2(byte - 127.0)
    codes = (blocks / scale).astype(np.float32).astype(dtype).astype(np.float64)
    return np.moveaxis((codes * scale).reshape(v.shape), -1, axis)


WIDE = False


def mx_kscale(k):
    if not WIDE:
        return np.ones(k)
    levels = np.array([10, -10, 5, -5, 0])
    if k % 512:
        return np.exp2(np.random.permutation(np.resize(levels, k // 32))).repeat(32)
    a = np.empty((k // 512, 16))
    for p in range(k // 512):
        a[p, :8] = np.random.permutation(np.resize(levels, 8))
        for g in range(8):
            far = levels[np.abs(levels - a[p, g]) >= 10]
            a[p, g + 8] = far[np.random.randint(len(far))]
    return np.exp2(a.ravel()).repeat(32)


def f64(x):
    return np.asarray(x).astype(np.float64)


E2M1 = np.array([0.0, 0.5, 1.0, 1.5, 2.0, 3.0, 4.0, 6.0, -0.0, -0.5, -1.0, -1.5, -2.0, -3.0, -4.0, -6.0])


def pack_weight(w, fmt):
    k, n = w.shape
    w = f64(np.asarray(w, np.float32).astype(ml_dtypes.bfloat16)).reshape(k // 32, 32, n)
    amax = np.abs(w).max(1)
    if fmt == "e4m3":
        byte = np.frexp(amax)[1] - 1 + 127 - 7
    else:
        mant, ex = np.frexp(amax / 6.0)
        byte = np.where(mant > 0.5, ex, ex - 1) + 127
    byte = np.clip(np.where(amax > 0, byte, 1), 1, 254)
    scaled = (w * np.exp2(127.0 - byte)[:, None, :]).reshape(k, n).astype(np.float32)
    by_word = np.ascontiguousarray(scaled.reshape(k // 512, 128, 4, n).transpose(0, 1, 3, 2))
    if fmt == "e4m3":
        words = by_word.astype(ml_dtypes.float8_e4m3fn).view(np.uint8)
    else:
        c = by_word.astype(ml_dtypes.float4_e2m1fn).view(np.uint8) & 0xF
        words = (c[..., 0::2] | (c[..., 1::2] << 4)).reshape(k // 512, 128, 2 * n)
    return np.ascontiguousarray(words), np.ascontiguousarray(byte.astype(np.uint8).reshape(k // 512, 16, n))


def unpack_weight(words, scales, fmt):
    g, _, n = scales.shape
    words = np.ascontiguousarray(words).reshape(g, 128, n, -1)
    if fmt == "e4m3":
        vals = words.view(ml_dtypes.float8_e4m3fn).astype(np.float64)
    else:
        nib = np.empty((g, 128, n, 4), np.uint8)
        nib[..., 0::2] = words & 0xF
        nib[..., 1::2] = words >> 4
        vals = E2M1[nib]
    vals = vals * np.repeat(np.exp2(scales.astype(np.float64) - 127.0), 8, axis=1)[..., None]
    return vals.transpose(0, 1, 3, 2).reshape(g * 512, n)


def planes(y):
    n, m = y.shape
    v = y.astype(np.float32).astype(ml_dtypes.bfloat16).astype(np.float64).reshape(n // 32, 32, m)
    top = np.abs(v).max(1)
    byte = np.clip(np.where(top > 0, np.frexp(top)[1] - 1 + 127 - 7, 1), 1, 254)
    codes = (v * np.exp2(127.0 - byte)[:, None, :]).reshape(n, m).astype(np.float32).astype(ml_dtypes.float8_e4m3fn).view(np.uint8)
    words = codes.reshape(n // 512, 128, 4, m).transpose(0, 1, 3, 2)
    return np.ascontiguousarray(words), np.ascontiguousarray(byte.astype(np.uint8).reshape(n // 512, 16, m))


def gelu(v):
    return 0.5 * v * (1.0 + np.tanh(np.sqrt(2.0 / np.pi) * (v + 0.044715 * v**3)))


K, M, T = 2048, 512, 1024


def setup_inputs():
    n = np.random.standard_normal
    s = mx_kscale(K)[:, None]
    x = n((K, T)) * s
    x4 = pack_weight(x, "e2m1")
    rest = x - unpack_weight(*x4, "e2m1")
    p_w4 = pack_weight(n((K, M)) / np.sqrt(K) / s, "e2m1")
    return {
        "x4_words": x4[0],
        "x4_scales": x4[1],
        "xr": (rest).astype(np.float32),
        "w4_words": p_w4[0],
        "w4_scales": p_w4[1],
        "b": (0.3 * n(512)).astype(np.float32),
    }


def reference(x4_words, x4_scales, xr, w4_words, w4_scales, b):
    x4_ = unpack_weight(x4_words, x4_scales, "e2m1")
    xr_ = mxq(f64(xr), 0, "e4m3")
    w4_ = unpack_weight(w4_words, w4_scales, "e2m1")
    y = w4_.T @ x4_ + w4_.T @ xr_
    out_0 = gelu(y + f64(b)[:, None])
    return (out_0,) + planes(out_0)

@@ -1,0 +1,205 @@
+from contextlib import ExitStack
+
+import concourse.mybir as mybir
+
+K, M, T = 2048, 512, 1024
+FLOPS = 2 * 2 * K * M * T
+
+F32 = mybir.dt.float32
+BF16 = mybir.dt.bfloat16
+I32 = mybir.dt.int32
+U32 = mybir.dt.uint32
+U8 = mybir.dt.uint8
+FP8X4 = mybir.dt.float8_e4m3fn_x4
+FP4X4 = mybir.dt.float4_e2m1fn_x4
+GELU = mybir.ActivationFunctionType.Gelu_apprx_tanh
+
+P = 128
+PACK = 4
+PASSES = K // (P * PACK)
+HALF = 512
+QUARTER = 256
+SCALAR_COLS = 192
+
+
+def interleave(copy, dst, src):
+    copy(
+        out=dst.rearrange("p (c i) j -> p c j i", i=4),
+        in_=src.rearrange("p j (c i) -> p c j i", i=4),
+    )
+
+
+def tile_mix_xres_fm_pl_gelu_kernel(
+    tc, x4_words, x4_scales, xr, w4_words, w4_scales, b, out_0, out_1, out_2
+):
+    nc = tc.nc
+    with ExitStack() as ctx:
+        sb = ctx.enter_context(tc.tile_pool(name="sb", bufs=1))
+        ps = ctx.enter_context(tc.psum_pool(name="ps", bufs=1))
+        ctx.enter_context(tc.manual_schedule())
+
+        w_raw = sb.tile([P, PASSES, 2 * M], U8, align_bytes=64)
+        ws_raw = sb.tile([P, PASSES, M], U8, align_bytes=64)
+        w_codes = [sb.tile([P, 2 * M], U8, align_bytes=64, name=f"w_codes{a}") for a in range(PASSES)]
+        w_scales = [sb.tile([P, M], U8, align_bytes=64, name=f"w_scales{a}") for a in range(PASSES)]
+        x4_codes = sb.tile([P, PASSES, 2 * T], U8, align_bytes=64)
+        x4_planes = sb.tile([P, PASSES, T], U8, align_bytes=64)
+        bias = sb.tile([P, PACK], F32)
+        pieces = [(a, h) for a in range(PASSES) for h in range(2)]
+        grouped = {k: sb.tile([P, HALF, PACK], BF16, align_bytes=64, name=f"grouped{k[0]}{k[1]}") for k in pieces}
+        xr_codes = {k: sb.tile([P, HALF], U32, align_bytes=64, name=f"xr_codes{k[0]}{k[1]}") for k in pieces}
+        xr_scales = {k: sb.tile([P, HALF], U8, align_bytes=64, name=f"xr_scales{k[0]}{k[1]}") for k in pieces}
+        acc = {
+            (h, r): ps.tile([P, HALF], F32, name=f"acc{h}{r}") for h in range(2) for r in range(PACK)
+        }
+        result = [sb.tile([P, PACK, HALF], F32, name=f"result{h}") for h in range(2)]
+        rounded = [sb.tile([P, QUARTER, PACK], BF16, align_bytes=64, name=f"rounded{q}") for q in range(4)]
+        out_codes = sb.tile([P, T], U32, align_bytes=64)
+        out_scales = sb.tile([P, T], U8, align_bytes=64)
+
+        nc.vector.memset(ws_raw[:].bitcast(I32), 0)
+        nc.vector.memset(x4_planes[:].bitcast(I32), 0)
+
+        nc.sync.dma_start(out=w_raw[:].bitcast(I32), in_=w4_words.rearrange("a p n -> p a n").bitcast(I32))
+        for q in range(4):
+            nc.sync.dma_start(
+                out=ws_raw[32 * q : 32 * q + 4].bitcast(I32),
+                in_=w4_scales[:, 4 * q : 4 * q + 4, :].rearrange("a r n -> r a n").bitcast(I32),
+            )
+
+        def load_x4_scales(q):
+            nc.sync.dma_start(
+                out=x4_planes[32 * q : 32 * q + 4].bitcast(I32),
+                in_=x4_scales[:, 4 * q : 4 * q + 4, :].rearrange("a r t -> r a t").bitcast(I32),
+            )
+
+        load_x4_scales(0)
+        load_x4_scales(1)
+        nc.sync.dma_start(out=x4_codes[:].bitcast(I32), in_=x4_words.rearrange("a p n -> p a n").bitcast(I32))
+        load_x4_scales(2)
+        load_x4_scales(3)
+        xr_rows = xr.rearrange("(a p j) t -> a p j t", p=P, j=PACK)
+        raw = {}
+        for a in (0, 1):
+            whole = sb.tile([P, PACK, T], F32, name=f"raw{a}")
+            nc.sync.dma_start(out=whole[:], in_=xr_rows[a])
+            for h in range(2):
+                raw[a, h] = whole[:, :, h * HALF : (h + 1) * HALF]
+        nc.sync.dma_start(out=bias[:], in_=b.rearrange("(p r) -> p r", r=PACK))
+        for h in range(2):
+            for a in (2, 3):
+                part = sb.tile([P, PACK, HALF], F32, name=f"raw{a}{h}")
+                nc.sync.dma_start(out=part[:], in_=xr_rows[a][:, :, h * HALF : (h + 1) * HALF])
+                raw[a, h] = part[:]
+
+        for a in range(PASSES):
+            nc.vector.tensor_copy(
+                out=w_codes[a][:].rearrange("p (r m e) -> p r m e", r=PACK, e=2),
+                in_=w_raw[:, a, :].rearrange("p (m r e) -> p r m e", r=PACK, e=2),
+            )
+            nc.vector.tensor_copy(
+                out=w_scales[a][:].rearrange("p (r m) -> p r m", r=PACK),
+                in_=ws_raw[:, a, :].rearrange("p (m r) -> p r m", r=PACK),
+            )
+
+        def group(piece, on_scalar):
+            if on_scalar:
+                interleave(nc.scalar.copy, grouped[piece][:, :on_scalar, :], raw[piece][:, :, :on_scalar])
+            interleave(nc.vector.tensor_copy, grouped[piece][:, on_scalar:, :], raw[piece][:, :, on_scalar:])
+
+        def quantize(piece):
+            nc.vector.quantize_mx(
+                out=xr_codes[piece][:].bitcast(FP8X4),
+                scales=xr_scales[piece][:],
+                in_=grouped[piece][:].rearrange("p t j -> p (t j)"),
+            )
+
+        def multiply(h, a, rhs, rhs_scale, start, stop):
+            for r in range(PACK):
+                nc.tensor.matmul_mx(
+                    out=acc[h, r][:],
+                    lhsT=w_codes[a][:, 2 * P * r : 2 * P * (r + 1)].bitcast(FP4X4),
+                    lhsT_scale=w_scales[a][:, P * r : P * (r + 1)],
+                    rhs=rhs,
+                    rhs_scale=rhs_scale,
+                    start=start,
+                    stop=stop,
+                )
+
+        def multiply_x4(a, h):
+            multiply(
+                h,
+                a,
+                x4_codes[:, a, 2 * HALF * h : 2 * HALF * (h + 1)].bitcast(FP4X4),
+                x4_planes[:, a, HALF * h : HALF * (h + 1)],
+                a == 0,
+                False,
+            )
+
+        def multiply_xr(a, h):
+            multiply(h, a, xr_codes[a, h][:].bitcast(FP8X4), xr_scales[a, h][:], False, a == PASSES - 1)
+
+        def activate(h):
+            for c in range(2):
+                cols = slice(c * QUARTER, (c + 1) * QUARTER)
+                for r in range(PACK):
+                    nc.scalar.activation(
+                        out=result[h][:, r, cols], in_=acc[h, r][:, cols], func=GELU, bias=bias[:, r : r + 1]
+                    )
+
+        def round_quarter(q):
+            cols = slice((q % 2) * QUARTER, (q % 2 + 1) * QUARTER)
+            interleave(nc.vector.tensor_copy, rounded[q][:], result[q // 2][:, :, cols])
+
+        def quantize_quarter(q):
+            cols = slice(q * QUARTER, (q + 1) * QUARTER)
+            nc.vector.quantize_mx(
+                out=out_codes[:, cols].bitcast(FP8X4),
+                scales=out_scales[:, cols],
+                in_=rounded[q][:].rearrange("p t j -> p (t j)"),
+            )
+
+        for a in range(PASSES):
+            multiply_x4(a, 0)
+        for a in (0, 1):
+            group((a, 0), SCALAR_COLS)
+            group((a, 1), SCALAR_COLS)
+            quantize((a, 0))
+            quantize((a, 1))
+            multiply_xr(a, 0)
+            multiply_x4(a, 1)
+            multiply_xr(a, 1)
+        for a in (2, 3):
+            group((a, 0), SCALAR_COLS)
+            quantize((a, 0))
+            multiply_xr(a, 0)
+            multiply_x4(a, 1)
+        activate(0)
+        group((2, 1), 0)
+        round_quarter(0)
+        quantize((2, 1))
+        multiply_xr(2, 1)
+        group((3, 1), SCALAR_COLS)
+        quantize((3, 1))
+        multiply_xr(3, 1)
+        activate(1)
+        quantize_quarter(0)
+        round_quarter(1)
+        round_quarter(2)
+        quantize_quarter(1)
+        quantize_quarter(2)
+        round_quarter(3)
+        quantize_quarter(3)
+
+        rows = out_0.rearrange("(p r) t -> p r t", r=PACK)
+        words = out_1[0].rearrange("p t i -> p (t i)").bitcast(I32)
+        nc.sync.dma_start(out=rows[:, :, :HALF], in_=result[0][:])
+        for r in range(PACK):
+            nc.sync.dma_start(out=rows[:, r, HALF:], in_=result[1][:, r, :])
+        nc.sync.dma_start(out=words[:, : 3 * QUARTER], in_=out_codes[:, : 3 * QUARTER].bitcast(I32))
+        nc.sync.dma_start(out=words[:, 3 * QUARTER :], in_=out_codes[:, 3 * QUARTER :].bitcast(I32))
+        for q in range(4):
+            nc.scalar.dma_start(
+                out=out_2[0, 4 * q : 4 * q + 4, :].bitcast(I32),
+                in_=out_scales[32 * q : 32 * q + 4, :].bitcast(I32),
+            )

@@ -53,7 +53,7 @@ def tile_mix_xres_fm_pl_gelu_kernel(
             (h, r): ps.tile([P, HALF], F32, name=f"acc{h}{r}") for h in range(2) for r in range(PACK)
         }
         result = [sb.tile([P, PACK, HALF], F32, name=f"result{h}") for h in range(2)]
-        rounded = [sb.tile([P, QUARTER, PACK], BF16, align_bytes=64, name=f"rounded{q}") for q in range(4)]
+        rounded = [sb.tile([P, HALF, PACK], BF16, align_bytes=64, name=f"rounded{h}") for h in range(2)]
         out_codes = sb.tile([P, T], U32, align_bytes=64)
         out_scales = sb.tile([P, T], U8, align_bytes=64)
 
@@ -61,23 +61,15 @@ def tile_mix_xres_fm_pl_gelu_kernel(
         nc.vector.memset(x4_planes[:].bitcast(I32), 0)
 
         nc.sync.dma_start(out=w_raw[:].bitcast(I32), in_=w4_words.rearrange("a p n -> p a n").bitcast(I32))
-        for q in range(4):
-            nc.sync.dma_start(
-                out=ws_raw[32 * q : 32 * q + 4].bitcast(I32),
-                in_=w4_scales[:, 4 * q : 4 * q + 4, :].rearrange("a r n -> r a n").bitcast(I32),
-            )
-
-        def load_x4_scales(q):
-            nc.sync.dma_start(
-                out=x4_planes[32 * q : 32 * q + 4].bitcast(I32),
-                in_=x4_scales[:, 4 * q : 4 * q + 4, :].rearrange("a r t -> r a t").bitcast(I32),
-            )
-
-        load_x4_scales(0)
-        load_x4_scales(1)
-        nc.sync.dma_start(out=x4_codes[:].bitcast(I32), in_=x4_words.rearrange("a p n -> p a n").bitcast(I32))
-        load_x4_scales(2)
-        load_x4_scales(3)
+        for plane, scales in ((ws_raw, w4_scales), (x4_planes, x4_scales)):
+            for r in range(4):
+                nc.sync.dma_start(
+                    out=plane[r:P:32].bitcast(I32),
+                    in_=scales.rearrange("a (q r) n -> r q a n", r=4)[r].bitcast(I32),
+                )
+        x4_rows = x4_words.rearrange("a p n -> p a n").bitcast(I32)
+        nc.sync.dma_start(out=x4_codes[:, :1, :].bitcast(I32), in_=x4_rows[:, :1, :])
+        nc.sync.dma_start(out=x4_codes[:, 1:, :].bitcast(I32), in_=x4_rows[:, 1:, :])
         xr_rows = xr.rearrange("(a p j) t -> a p j t", p=P, j=PACK)
         raw = {}
         for a in (0, 1):
@@ -89,7 +81,9 @@ def tile_mix_xres_fm_pl_gelu_kernel(
         for h in range(2):
             for a in (2, 3):
                 part = sb.tile([P, PACK, HALF], F32, name=f"raw{a}{h}")
-                nc.sync.dma_start(out=part[:], in_=xr_rows[a][:, :, h * HALF : (h + 1) * HALF])
+                cuts = (0, QUARTER, HALF) if (a, h) == (3, 1) else (0, HALF)
+                for lo, hi in zip(cuts, cuts[1:]):
+                    nc.sync.dma_start(out=part[:, :, lo:hi], in_=xr_rows[a][:, :, h * HALF + lo : h * HALF + hi])
                 raw[a, h] = part[:]
 
         for a in range(PASSES):
@@ -102,16 +96,18 @@ def tile_mix_xres_fm_pl_gelu_kernel(
                 in_=ws_raw[:, a, :].rearrange("p (m r) -> p r m", r=PACK),
             )
 
-        def group(piece, on_scalar):
-            if on_scalar:
-                interleave(nc.scalar.copy, grouped[piece][:, :on_scalar, :], raw[piece][:, :, :on_scalar])
-            interleave(nc.vector.tensor_copy, grouped[piece][:, on_scalar:, :], raw[piece][:, :, on_scalar:])
+        def group(copy, piece, lo, hi):
+            interleave(copy, grouped[piece][:, lo:hi, :], raw[piece][:, :, lo:hi])
 
-        def quantize(piece):
+        def group_shared(piece):
+            group(nc.scalar.copy, piece, 0, SCALAR_COLS)
+            group(nc.vector.tensor_copy, piece, SCALAR_COLS, HALF)
+
+        def quantize(piece, lo=0, hi=HALF):
             nc.vector.quantize_mx(
-                out=xr_codes[piece][:].bitcast(FP8X4),
-                scales=xr_scales[piece][:],
-                in_=grouped[piece][:].rearrange("p t j -> p (t j)"),
+                out=xr_codes[piece][:, lo:hi].bitcast(FP8X4),
+                scales=xr_scales[piece][:, lo:hi],
+                in_=grouped[piece][:, lo:hi, :].rearrange("p t j -> p (t j)"),
             )
 
         def multiply(h, a, rhs, rhs_scale, start, stop):
@@ -139,67 +135,73 @@ def tile_mix_xres_fm_pl_gelu_kernel(
         def multiply_xr(a, h):
             multiply(h, a, xr_codes[a, h][:].bitcast(FP8X4), xr_scales[a, h][:], False, a == PASSES - 1)
 
-        def activate(h):
-            for c in range(2):
-                cols = slice(c * QUARTER, (c + 1) * QUARTER)
-                for r in range(PACK):
-                    nc.scalar.activation(
-                        out=result[h][:, r, cols], in_=acc[h, r][:, cols], func=GELU, bias=bias[:, r : r + 1]
-                    )
+        def activate(h, r, lo, hi):
+            nc.scalar.activation(
+                out=result[h][:, r, lo:hi], in_=acc[h, r][:, lo:hi], func=GELU, bias=bias[:, r : r + 1]
+            )
 
-        def round_quarter(q):
-            cols = slice((q % 2) * QUARTER, (q % 2 + 1) * QUARTER)
-            interleave(nc.vector.tensor_copy, rounded[q][:], result[q // 2][:, :, cols])
+        def round_result(copy, h, lo, hi):
+            interleave(copy, rounded[h][:, lo:hi, :], result[h][:, :, lo:hi])
 
-        def quantize_quarter(q):
-            cols = slice(q * QUARTER, (q + 1) * QUARTER)
+        def quantize_result(h):
+            cols = slice(h * HALF, (h + 1) * HALF)
             nc.vector.quantize_mx(
                 out=out_codes[:, cols].bitcast(FP8X4),
                 scales=out_scales[:, cols],
-                in_=rounded[q][:].rearrange("p t j -> p (t j)"),
+                in_=rounded[h][:].rearrange("p t j -> p (t j)"),
             )
 
-        for a in range(PASSES):
+        multiply_x4(0, 0)
+        multiply_x4(0, 1)
+        for a in (1, 2, 3):
             multiply_x4(a, 0)
         for a in (0, 1):
-            group((a, 0), SCALAR_COLS)
-            group((a, 1), SCALAR_COLS)
+            multiply_x4(a + 1, 1)
+            group_shared((a, 0))
+            group_shared((a, 1))
             quantize((a, 0))
             quantize((a, 1))
             multiply_xr(a, 0)
-            multiply_x4(a, 1)
             multiply_xr(a, 1)
         for a in (2, 3):
-            group((a, 0), SCALAR_COLS)
+            group_shared((a, 0))
             quantize((a, 0))
             multiply_xr(a, 0)
-            multiply_x4(a, 1)
-        activate(0)
-        group((2, 1), 0)
-        round_quarter(0)
+        multiply_x4(3, 1)
+        for r in range(PACK):
+            activate(0, r, 0, HALF)
+        group(nc.vector.tensor_copy, (2, 1), 0, HALF)
         quantize((2, 1))
         multiply_xr(2, 1)
-        group((3, 1), SCALAR_COLS)
-        quantize((3, 1))
+        group(nc.scalar.copy, (3, 1), 0, 128)
+        group(nc.vector.tensor_copy, (3, 1), 128, QUARTER)
+        group(nc.scalar.copy, (3, 1), QUARTER, QUARTER + 96)
+        quantize((3, 1), 0, QUARTER)
+        group(nc.vector.tensor_copy, (3, 1), QUARTER + 96, HALF)
+        quantize((3, 1), QUARTER, HALF)
         multiply_xr(3, 1)
-        activate(1)
-        quantize_quarter(0)
-        round_quarter(1)
-        round_quarter(2)
-        quantize_quarter(1)
-        quantize_quarter(2)
-        round_quarter(3)
-        quantize_quarter(3)
+        activate(1, 0, 0, HALF)
+        activate(1, 1, 0, HALF)
+        for lo in (0, QUARTER):
+            activate(1, 2, lo, lo + QUARTER)
+            activate(1, 3, lo, lo + QUARTER)
+        round_result(nc.vector.tensor_copy, 0, 0, HALF)
+        quantize_result(0)
+        round_result(nc.vector.tensor_copy, 1, 0, QUARTER)
+        round_result(nc.vector.tensor_copy, 1, QUARTER, HALF - 96)
+        round_result(nc.scalar.copy, 1, HALF - 96, HALF)
+        quantize_result(1)
 
         rows = out_0.rearrange("(p r) t -> p r t", r=PACK)
         words = out_1[0].rearrange("p t i -> p (t i)").bitcast(I32)
         nc.sync.dma_start(out=rows[:, :, :HALF], in_=result[0][:])
         for r in range(PACK):
             nc.sync.dma_start(out=rows[:, r, HALF:], in_=result[1][:, r, :])
-        nc.sync.dma_start(out=words[:, : 3 * QUARTER], in_=out_codes[:, : 3 * QUARTER].bitcast(I32))
-        nc.sync.dma_start(out=words[:, 3 * QUARTER :], in_=out_codes[:, 3 * QUARTER :].bitcast(I32))
-        for q in range(4):
+            if r == 1:
+                nc.sync.dma_start(out=words[:, :HALF], in_=out_codes[:, :HALF].bitcast(I32))
+        nc.sync.dma_start(out=words[:, HALF:], in_=out_codes[:, HALF:].bitcast(I32))
+        for r in range(4):
             nc.scalar.dma_start(
-                out=out_2[0, 4 * q : 4 * q + 4, :].bitcast(I32),
-                in_=out_scales[32 * q : 32 * q + 4, :].bitcast(I32),
+                out=out_2[0].rearrange("(q r) t -> r q t", r=4)[r].bitcast(I32),
+                in_=out_scales[r:P:32, :].bitcast(I32),
             )

@@ -57,13 +57,13 @@ def tile_mix_xres_fm_pl_gelu_kernel(
         out_codes = sb.tile([P, T], U32, align_bytes=64)
         out_scales = sb.tile([P, T], U8, align_bytes=64)
 
-        nc.vector.memset(ws_raw[:].bitcast(I32), 0)
         nc.vector.memset(x4_planes[:].bitcast(I32), 0)
+        nc.vector.memset(ws_raw[:].bitcast(I32), 0)
 
         nc.sync.dma_start(out=w_raw[:].bitcast(I32), in_=w4_words.rearrange("a p n -> p a n").bitcast(I32))
-        for plane, scales in ((ws_raw, w4_scales), (x4_planes, x4_scales)):
+        for queue, plane, scales in ((nc.sync, ws_raw, w4_scales), (nc.gpsimd, x4_planes, x4_scales)):
             for r in range(4):
-                nc.sync.dma_start(
+                queue.dma_start(
                     out=plane[r:P:32].bitcast(I32),
                     in_=scales.rearrange("a (q r) n -> r q a n", r=4)[r].bitcast(I32),
                 )
@@ -72,14 +72,15 @@ def tile_mix_xres_fm_pl_gelu_kernel(
         nc.sync.dma_start(out=x4_codes[:, 1:, :].bitcast(I32), in_=x4_rows[:, 1:, :])
         xr_rows = xr.rearrange("(a p j) t -> a p j t", p=P, j=PACK)
         raw = {}
-        for a in (0, 1):
+        for a in (0,):
             whole = sb.tile([P, PACK, T], F32, name=f"raw{a}")
             nc.sync.dma_start(out=whole[:], in_=xr_rows[a])
             for h in range(2):
                 raw[a, h] = whole[:, :, h * HALF : (h + 1) * HALF]
-        nc.sync.dma_start(out=bias[:], in_=b.rearrange("(p r) -> p r", r=PACK))
         for h in range(2):
-            for a in (2, 3):
+            if h == 1:
+                nc.sync.dma_start(out=bias[:], in_=b.rearrange("(p r) -> p r", r=PACK))
+            for a in (1, 2, 3):
                 part = sb.tile([P, PACK, HALF], F32, name=f"raw{a}{h}")
                 cuts = (0, QUARTER, HALF) if (a, h) == (3, 1) else (0, HALF)
                 for lo, hi in zip(cuts, cuts[1:]):
@@ -143,65 +144,72 @@ def tile_mix_xres_fm_pl_gelu_kernel(
         def round_result(copy, h, lo, hi):
             interleave(copy, rounded[h][:, lo:hi, :], result[h][:, :, lo:hi])
 
-        def quantize_result(h):
-            cols = slice(h * HALF, (h + 1) * HALF)
+        def quantize_result(h, lo, hi):
+            cols = slice(h * HALF + lo, h * HALF + hi)
             nc.vector.quantize_mx(
                 out=out_codes[:, cols].bitcast(FP8X4),
                 scales=out_scales[:, cols],
-                in_=rounded[h][:].rearrange("p t j -> p (t j)"),
+                in_=rounded[h][:, lo:hi, :].rearrange("p t j -> p (t j)"),
             )
 
+        vec, act = nc.vector.tensor_copy, nc.scalar.copy
         multiply_x4(0, 0)
         multiply_x4(0, 1)
         for a in (1, 2, 3):
             multiply_x4(a, 0)
-        for a in (0, 1):
-            multiply_x4(a + 1, 1)
+        multiply_x4(1, 1)
+        group_shared((0, 0))
+        group_shared((0, 1))
+        quantize((0, 0))
+        quantize((0, 1))
+        multiply_xr(0, 0)
+        multiply_xr(0, 1)
+        for a in (1, 2, 3):
             group_shared((a, 0))
-            group_shared((a, 1))
-            quantize((a, 0))
-            quantize((a, 1))
-            multiply_xr(a, 0)
-            multiply_xr(a, 1)
-        for a in (2, 3):
-            group_shared((a, 0))
             quantize((a, 0))
             multiply_xr(a, 0)
-        multiply_x4(3, 1)
+        multiply_x4(2, 1)
         for r in range(PACK):
             activate(0, r, 0, HALF)
-        group(nc.vector.tensor_copy, (2, 1), 0, HALF)
+        group(vec, (1, 1), 0, HALF)
+        quantize((1, 1))
+        multiply_xr(1, 1)
+        multiply_x4(3, 1)
+        round_result(vec, 0, 0, QUARTER)
+        group(act, (2, 1), 0, QUARTER)
+        group(vec, (2, 1), QUARTER, HALF)
         quantize((2, 1))
         multiply_xr(2, 1)
-        group(nc.scalar.copy, (3, 1), 0, 128)
-        group(nc.vector.tensor_copy, (3, 1), 128, QUARTER)
-        group(nc.scalar.copy, (3, 1), QUARTER, QUARTER + 96)
+        round_result(act, 0, QUARTER, HALF)
+        group(vec, (3, 1), 0, QUARTER)
+        group(act, (3, 1), QUARTER, QUARTER + 96)
+        group(vec, (3, 1), QUARTER + 96, HALF)
         quantize((3, 1), 0, QUARTER)
-        group(nc.vector.tensor_copy, (3, 1), QUARTER + 96, HALF)
         quantize((3, 1), QUARTER, HALF)
+        quantize_result(0, 0, HALF)
         multiply_xr(3, 1)
         activate(1, 0, 0, HALF)
         activate(1, 1, 0, HALF)
         for lo in (0, QUARTER):
             activate(1, 2, lo, lo + QUARTER)
             activate(1, 3, lo, lo + QUARTER)
-        round_result(nc.vector.tensor_copy, 0, 0, HALF)
-        quantize_result(0)
-        round_result(nc.vector.tensor_copy, 1, 0, QUARTER)
-        round_result(nc.vector.tensor_copy, 1, QUARTER, HALF - 96)
-        round_result(nc.scalar.copy, 1, HALF - 96, HALF)
-        quantize_result(1)
+        round_result(vec, 1, 0, QUARTER)
+        round_result(vec, 1, QUARTER, HALF - 96)
+        round_result(act, 1, HALF - 96, HALF)
+        quantize_result(1, 0, QUARTER)
+        quantize_result(1, QUARTER, HALF)
 
         rows = out_0.rearrange("(p r) t -> p r t", r=PACK)
         words = out_1[0].rearrange("p t i -> p (t i)").bitcast(I32)
         nc.sync.dma_start(out=rows[:, :, :HALF], in_=result[0][:])
+        nc.sync.dma_start(out=words[:, :HALF], in_=out_codes[:, :HALF].bitcast(I32))
         for r in range(PACK):
             nc.sync.dma_start(out=rows[:, r, HALF:], in_=result[1][:, r, :])
-            if r == 1:
-                nc.sync.dma_start(out=words[:, :HALF], in_=out_codes[:, :HALF].bitcast(I32))
-        nc.sync.dma_start(out=words[:, HALF:], in_=out_codes[:, HALF:].bitcast(I32))
+        for lo in (HALF, HALF + QUARTER):
+            nc.sync.dma_start(out=words[:, lo : lo + QUARTER], in_=out_codes[:, lo : lo + QUARTER].bitcast(I32))
         for r in range(4):
-            nc.scalar.dma_start(
+            queue = nc.sync if r == 0 else nc.scalar
+            queue.dma_start(
                 out=out_2[0].rearrange("(q r) t -> r q t", r=4)[r].bitcast(I32),
                 in_=out_scales[r:P:32, :].bitcast(I32),
             )

@@ -57,18 +57,25 @@ def tile_mix_xres_fm_pl_gelu_kernel(
         out_codes = sb.tile([P, T], U32, align_bytes=64)
         out_scales = sb.tile([P, T], U8, align_bytes=64)
 
-        nc.vector.memset(x4_planes[:].bitcast(I32), 0)
         nc.vector.memset(ws_raw[:].bitcast(I32), 0)
+        nc.vector.memset(x4_planes[:].bitcast(I32), 0)
 
         nc.sync.dma_start(out=w_raw[:].bitcast(I32), in_=w4_words.rearrange("a p n -> p a n").bitcast(I32))
-        for queue, plane, scales in ((nc.sync, ws_raw, w4_scales), (nc.gpsimd, x4_planes, x4_scales)):
-            for r in range(4):
-                queue.dma_start(
-                    out=plane[r:P:32].bitcast(I32),
-                    in_=scales.rearrange("a (q r) n -> r q a n", r=4)[r].bitcast(I32),
-                )
+
+        def load_scale_rows(plane, scales, r):
+            nc.sync.dma_start(
+                out=plane[r:P:32].bitcast(I32),
+                in_=scales.rearrange("a (q r) n -> r q a n", r=4)[r].bitcast(I32),
+            )
+
+        for r in range(4):
+            load_scale_rows(ws_raw, w4_scales, r)
         x4_rows = x4_words.rearrange("a p n -> p a n").bitcast(I32)
+        load_scale_rows(x4_planes, x4_scales, 0)
+        load_scale_rows(x4_planes, x4_scales, 1)
         nc.sync.dma_start(out=x4_codes[:, :1, :].bitcast(I32), in_=x4_rows[:, :1, :])
+        load_scale_rows(x4_planes, x4_scales, 2)
+        load_scale_rows(x4_planes, x4_scales, 3)
         nc.sync.dma_start(out=x4_codes[:, 1:, :].bitcast(I32), in_=x4_rows[:, 1:, :])
         xr_rows = xr.rearrange("(a p j) t -> a p j t", p=P, j=PACK)
         raw = {}
@@ -168,19 +175,18 @@ def tile_mix_xres_fm_pl_gelu_kernel(
             group_shared((a, 0))
             quantize((a, 0))
             multiply_xr(a, 0)
-        multiply_x4(2, 1)
+            if a > 1:
+                multiply_x4(a, 1)
         for r in range(PACK):
             activate(0, r, 0, HALF)
         group(vec, (1, 1), 0, HALF)
         quantize((1, 1))
         multiply_xr(1, 1)
-        multiply_x4(3, 1)
-        round_result(vec, 0, 0, QUARTER)
-        group(act, (2, 1), 0, QUARTER)
-        group(vec, (2, 1), QUARTER, HALF)
+        group_shared((2, 1))
+        round_result(vec, 0, 320, HALF)
         quantize((2, 1))
         multiply_xr(2, 1)
-        round_result(act, 0, QUARTER, HALF)
+        round_result(act, 0, 0, 320)
         group(vec, (3, 1), 0, QUARTER)
         group(act, (3, 1), QUARTER, QUARTER + 96)
         group(vec, (3, 1), QUARTER + 96, HALF)

@@ -19,7 +19,7 @@ PACK = 4
 PASSES = K // (P * PACK)
 HALF = 512
 QUARTER = 256
-SCALAR_COLS = 192
+SCALAR_COLS = 224
 
 
 def interleave(copy, dst, src):
@@ -79,20 +79,16 @@ def tile_mix_xres_fm_pl_gelu_kernel(
         nc.sync.dma_start(out=x4_codes[:, 1:, :].bitcast(I32), in_=x4_rows[:, 1:, :])
         xr_rows = xr.rearrange("(a p j) t -> a p j t", p=P, j=PACK)
         raw = {}
-        for a in (0,):
+        for a in range(PASSES - 1):
             whole = sb.tile([P, PACK, T], F32, name=f"raw{a}")
             nc.sync.dma_start(out=whole[:], in_=xr_rows[a])
             for h in range(2):
                 raw[a, h] = whole[:, :, h * HALF : (h + 1) * HALF]
+        nc.sync.dma_start(out=bias[:], in_=b.rearrange("(p r) -> p r", r=PACK))
         for h in range(2):
-            if h == 1:
-                nc.sync.dma_start(out=bias[:], in_=b.rearrange("(p r) -> p r", r=PACK))
-            for a in (1, 2, 3):
-                part = sb.tile([P, PACK, HALF], F32, name=f"raw{a}{h}")
-                cuts = (0, QUARTER, HALF) if (a, h) == (3, 1) else (0, HALF)
-                for lo, hi in zip(cuts, cuts[1:]):
-                    nc.sync.dma_start(out=part[:, :, lo:hi], in_=xr_rows[a][:, :, h * HALF + lo : h * HALF + hi])
-                raw[a, h] = part[:]
+            part = sb.tile([P, PACK, HALF], F32, name=f"raw_last{h}")
+            nc.sync.dma_start(out=part[:], in_=xr_rows[PASSES - 1][:, :, h * HALF : (h + 1) * HALF])
+            raw[PASSES - 1, h] = part[:]
 
         for a in range(PASSES):
             nc.vector.tensor_copy(
@@ -165,33 +161,23 @@ def tile_mix_xres_fm_pl_gelu_kernel(
         for a in (1, 2, 3):
             multiply_x4(a, 0)
         multiply_x4(1, 1)
-        group_shared((0, 0))
-        group_shared((0, 1))
-        quantize((0, 0))
-        quantize((0, 1))
-        multiply_xr(0, 0)
-        multiply_xr(0, 1)
-        for a in (1, 2, 3):
+        for a in range(PASSES - 1):
             group_shared((a, 0))
+            group_shared((a, 1))
             quantize((a, 0))
+            quantize((a, 1))
             multiply_xr(a, 0)
-            if a > 1:
-                multiply_x4(a, 1)
+            multiply_xr(a, 1)
+            if a + 2 < PASSES:
+                multiply_x4(a + 2, 1)
+        group_shared((3, 0))
+        quantize((3, 0))
+        multiply_xr(3, 0)
         for r in range(PACK):
             activate(0, r, 0, HALF)
-        group(vec, (1, 1), 0, HALF)
-        quantize((1, 1))
-        multiply_xr(1, 1)
-        group_shared((2, 1))
-        round_result(vec, 0, 320, HALF)
-        quantize((2, 1))
-        multiply_xr(2, 1)
-        round_result(act, 0, 0, 320)
-        group(vec, (3, 1), 0, QUARTER)
-        group(act, (3, 1), QUARTER, QUARTER + 96)
-        group(vec, (3, 1), QUARTER + 96, HALF)
-        quantize((3, 1), 0, QUARTER)
-        quantize((3, 1), QUARTER, HALF)
+        group(vec, (3, 1), 0, HALF)
+        quantize((3, 1))
+        round_result(vec, 0, 0, HALF)
         quantize_result(0, 0, HALF)
         multiply_xr(3, 1)
         activate(1, 0, 0, HALF)
@@ -207,10 +193,12 @@ def tile_mix_xres_fm_pl_gelu_kernel(
 
         rows = out_0.rearrange("(p r) t -> p r t", r=PACK)
         words = out_1[0].rearrange("p t i -> p (t i)").bitcast(I32)
-        nc.sync.dma_start(out=rows[:, :, :HALF], in_=result[0][:])
-        nc.sync.dma_start(out=words[:, :HALF], in_=out_codes[:, :HALF].bitcast(I32))
+        for r in range(PACK):
+            nc.sync.dma_start(out=rows[:, r, :HALF], in_=result[0][:, r, :])
         for r in range(PACK):
             nc.sync.dma_start(out=rows[:, r, HALF:], in_=result[1][:, r, :])
+            if r == 1:
+                nc.sync.dma_start(out=words[:, :HALF], in_=out_codes[:, :HALF].bitcast(I32))
         for lo in (HALF, HALF + QUARTER):
             nc.sync.dma_start(out=words[:, lo : lo + QUARTER], in_=out_codes[:, lo : lo + QUARTER].bitcast(I32))
         for r in range(4):

@@ -9,6 +9,7 @@ F32 = mybir.dt.float32
 BF16 = mybir.dt.bfloat16
 I32 = mybir.dt.int32
 U32 = mybir.dt.uint32
+U16 = mybir.dt.uint16
 U8 = mybir.dt.uint8
 FP8X4 = mybir.dt.float8_e4m3fn_x4
 FP4X4 = mybir.dt.float4_e2m1fn_x4
@@ -20,6 +21,7 @@ PASSES = K // (P * PACK)
 HALF = 512
 QUARTER = 256
 SCALAR_COLS = 224
+LAST = 384
 
 
 def interleave(copy, dst, src):
@@ -42,7 +44,8 @@ def tile_mix_xres_fm_pl_gelu_kernel(
         ws_raw = sb.tile([P, PASSES, M], U8, align_bytes=64)
         w_codes = [sb.tile([P, 2 * M], U8, align_bytes=64, name=f"w_codes{a}") for a in range(PASSES)]
         w_scales = [sb.tile([P, M], U8, align_bytes=64, name=f"w_scales{a}") for a in range(PASSES)]
-        x4_codes = sb.tile([P, PASSES, 2 * T], U8, align_bytes=64)
+        x4_codes = sb.tile([P, PASSES - 1, 2 * T], U8, align_bytes=64)
+        x4_last = [sb.tile([P, 2 * HALF], U8, align_bytes=64, name=f"x4_last{h}") for h in range(2)]
         x4_planes = sb.tile([P, PASSES, T], U8, align_bytes=64)
         bias = sb.tile([P, PACK], F32)
         pieces = [(a, h) for a in range(PASSES) for h in range(2)]
@@ -57,6 +60,9 @@ def tile_mix_xres_fm_pl_gelu_kernel(
         out_codes = sb.tile([P, T], U32, align_bytes=64)
         out_scales = sb.tile([P, T], U8, align_bytes=64)
 
+        warm = sb.tile([P, 8], F32)
+        nc.gpsimd.memset(warm[:], 0.0)
+        nc.scalar.activation(out=warm[:, 4:5], in_=warm[:, 0:1], func=GELU)
         nc.vector.memset(ws_raw[:].bitcast(I32), 0)
         nc.vector.memset(x4_planes[:].bitcast(I32), 0)
 
@@ -76,7 +82,7 @@ def tile_mix_xres_fm_pl_gelu_kernel(
         nc.sync.dma_start(out=x4_codes[:, :1, :].bitcast(I32), in_=x4_rows[:, :1, :])
         load_scale_rows(x4_planes, x4_scales, 2)
         load_scale_rows(x4_planes, x4_scales, 3)
-        nc.sync.dma_start(out=x4_codes[:, 1:, :].bitcast(I32), in_=x4_rows[:, 1:, :])
+        nc.sync.dma_start(out=x4_codes[:, 1:3, :].bitcast(I32), in_=x4_rows[:, 1:3, :])
         xr_rows = xr.rearrange("(a p j) t -> a p j t", p=P, j=PACK)
         raw = {}
         for a in range(PASSES - 1):
@@ -85,15 +91,17 @@ def tile_mix_xres_fm_pl_gelu_kernel(
             for h in range(2):
                 raw[a, h] = whole[:, :, h * HALF : (h + 1) * HALF]
         nc.sync.dma_start(out=bias[:], in_=b.rearrange("(p r) -> p r", r=PACK))
+        nc.sync.dma_start(out=x4_last[0][:].bitcast(I32), in_=x4_rows[:, 3, :QUARTER])
         for h in range(2):
             part = sb.tile([P, PACK, HALF], F32, name=f"raw_last{h}")
             nc.sync.dma_start(out=part[:], in_=xr_rows[PASSES - 1][:, :, h * HALF : (h + 1) * HALF])
             raw[PASSES - 1, h] = part[:]
+        nc.sync.dma_start(out=x4_last[1][:].bitcast(I32), in_=x4_rows[:, 3, QUARTER:])
 
         for a in range(PASSES):
             nc.vector.tensor_copy(
-                out=w_codes[a][:].rearrange("p (r m e) -> p r m e", r=PACK, e=2),
-                in_=w_raw[:, a, :].rearrange("p (m r e) -> p r m e", r=PACK, e=2),
+                out=w_codes[a][:].bitcast(U16).rearrange("p (r m) -> p r m", r=PACK),
+                in_=w_raw[:, a, :].bitcast(U16).rearrange("p (m r) -> p r m", r=PACK),
             )
             nc.vector.tensor_copy(
                 out=w_scales[a][:].rearrange("p (r m) -> p r m", r=PACK),
@@ -127,10 +135,11 @@ def tile_mix_xres_fm_pl_gelu_kernel(
                 )
 
         def multiply_x4(a, h):
+            codes = x4_last[h][:] if a == PASSES - 1 else x4_codes[:, a, 2 * HALF * h : 2 * HALF * (h + 1)]
             multiply(
                 h,
                 a,
-                x4_codes[:, a, 2 * HALF * h : 2 * HALF * (h + 1)].bitcast(FP4X4),
+                codes.bitcast(FP4X4),
                 x4_planes[:, a, HALF * h : HALF * (h + 1)],
                 a == 0,
                 False,
@@ -158,36 +167,45 @@ def tile_mix_xres_fm_pl_gelu_kernel(
         vec, act = nc.vector.tensor_copy, nc.scalar.copy
         multiply_x4(0, 0)
         multiply_x4(0, 1)
-        for a in (1, 2, 3):
+        for a in (1, 2):
             multiply_x4(a, 0)
-        multiply_x4(1, 1)
         for a in range(PASSES - 1):
             group_shared((a, 0))
             group_shared((a, 1))
             quantize((a, 0))
             quantize((a, 1))
+            if a == 2:
+                multiply_x4(3, 0)
             multiply_xr(a, 0)
             multiply_xr(a, 1)
-            if a + 2 < PASSES:
-                multiply_x4(a + 2, 1)
-        group_shared((3, 0))
-        quantize((3, 0))
+            if a < 2:
+                multiply_x4(a + 1, 1)
+        group(act, (3, 0), HALF - 192, HALF)
+        group(vec, (3, 0), 0, QUARTER)
+        group(vec, (3, 0), QUARTER, HALF - 192)
+        quantize((3, 0), 0, QUARTER)
+        quantize((3, 0), QUARTER, HALF)
         multiply_xr(3, 0)
         for r in range(PACK):
             activate(0, r, 0, HALF)
-        group(vec, (3, 1), 0, HALF)
-        quantize((3, 1))
-        round_result(vec, 0, 0, HALF)
-        quantize_result(0, 0, HALF)
+        group(vec, (3, 1), 0, QUARTER)
+        group(vec, (3, 1), QUARTER, HALF)
+        quantize((3, 1), 0, QUARTER)
+        quantize((3, 1), QUARTER, HALF)
+        round_result(vec, 0, 0, QUARTER)
+        round_result(vec, 0, QUARTER, HALF)
+        quantize_result(0, 0, QUARTER)
+        quantize_result(0, QUARTER, HALF)
+        multiply_x4(3, 1)
         multiply_xr(3, 1)
         activate(1, 0, 0, HALF)
         activate(1, 1, 0, HALF)
-        for lo in (0, QUARTER):
-            activate(1, 2, lo, lo + QUARTER)
-            activate(1, 3, lo, lo + QUARTER)
+        for lo, hi in ((0, QUARTER), (QUARTER, LAST), (LAST, HALF)):
+            activate(1, 2, lo, hi)
+            activate(1, 3, lo, hi)
         round_result(vec, 1, 0, QUARTER)
-        round_result(vec, 1, QUARTER, HALF - 96)
-        round_result(act, 1, HALF - 96, HALF)
+        round_result(vec, 1, QUARTER, LAST)
+        round_result(act, 1, LAST, HALF)
         quantize_result(1, 0, QUARTER)
         quantize_result(1, QUARTER, HALF)
 
@@ -195,12 +213,12 @@ def tile_mix_xres_fm_pl_gelu_kernel(
         words = out_1[0].rearrange("p t i -> p (t i)").bitcast(I32)
         for r in range(PACK):
             nc.sync.dma_start(out=rows[:, r, :HALF], in_=result[0][:, r, :])
-        for r in range(PACK):
+        for r in range(2):
             nc.sync.dma_start(out=rows[:, r, HALF:], in_=result[1][:, r, :])
-            if r == 1:
-                nc.sync.dma_start(out=words[:, :HALF], in_=out_codes[:, :HALF].bitcast(I32))
-        for lo in (HALF, HALF + QUARTER):
-            nc.sync.dma_start(out=words[:, lo : lo + QUARTER], in_=out_codes[:, lo : lo + QUARTER].bitcast(I32))
+        nc.sync.dma_start(out=words[:, :HALF], in_=out_codes[:, :HALF].bitcast(I32))
+        nc.sync.dma_start(out=rows[:, 2:, HALF:], in_=result[1][:, 2:, :])
+        for lo, hi in ((HALF, HALF + QUARTER), (HALF + QUARTER, T)):
+            nc.sync.dma_start(out=words[:, lo:hi], in_=out_codes[:, lo:hi].bitcast(I32))
         for r in range(4):
             queue = nc.sync if r == 0 else nc.scalar
             queue.dma_start(

@@ -77,12 +77,10 @@ def tile_mix_xres_fm_pl_gelu_kernel(
         for r in range(4):
             load_scale_rows(ws_raw, w4_scales, r)
         x4_rows = x4_words.rearrange("a p n -> p a n").bitcast(I32)
-        load_scale_rows(x4_planes, x4_scales, 0)
-        load_scale_rows(x4_planes, x4_scales, 1)
-        nc.sync.dma_start(out=x4_codes[:, :1, :].bitcast(I32), in_=x4_rows[:, :1, :])
-        load_scale_rows(x4_planes, x4_scales, 2)
-        load_scale_rows(x4_planes, x4_scales, 3)
-        nc.sync.dma_start(out=x4_codes[:, 1:3, :].bitcast(I32), in_=x4_rows[:, 1:3, :])
+        nc.sync.dma_start(out=x4_codes[:, :2, :].bitcast(I32), in_=x4_rows[:, :2, :])
+        for r in range(4):
+            load_scale_rows(x4_planes, x4_scales, r)
+        nc.sync.dma_start(out=x4_codes[:, 2:3, :].bitcast(I32), in_=x4_rows[:, 2:3, :])
         xr_rows = xr.rearrange("(a p j) t -> a p j t", p=P, j=PACK)
         raw = {}
         for a in range(PASSES - 1):

@@ -47,7 +47,9 @@ def tile_mix_xres_fm_pl_gelu_kernel(
         x4_codes = sb.tile([P, PASSES - 1, 2 * T], U8, align_bytes=64)
         x4_last = [sb.tile([P, 2 * HALF], U8, align_bytes=64, name=f"x4_last{h}") for h in range(2)]
         x4_planes = sb.tile([P, PASSES, T], U8, align_bytes=64)
-        bias = sb.tile([P, PACK], F32)
+        bias_row = sb.tile([P, P], F32, align_bytes=64)
+        bias_dealt = sb.tile([P, P], F32, align_bytes=64)
+        bias = sb.tile([P, P], F32, align_bytes=64)
         pieces = [(a, h) for a in range(PASSES) for h in range(2)]
         grouped = {k: sb.tile([P, HALF, PACK], BF16, align_bytes=64, name=f"grouped{k[0]}{k[1]}") for k in pieces}
         xr_codes = {k: sb.tile([P, HALF], U32, align_bytes=64, name=f"xr_codes{k[0]}{k[1]}") for k in pieces}
@@ -65,6 +67,7 @@ def tile_mix_xres_fm_pl_gelu_kernel(
         nc.scalar.activation(out=warm[:, 4:5], in_=warm[:, 0:1], func=GELU)
         nc.vector.memset(ws_raw[:].bitcast(I32), 0)
         nc.vector.memset(x4_planes[:].bitcast(I32), 0)
+        nc.vector.memset(bias_row[:], 0.0)
 
         nc.sync.dma_start(out=w_raw[:].bitcast(I32), in_=w4_words.rearrange("a p n -> p a n").bitcast(I32))
 
@@ -86,9 +89,10 @@ def tile_mix_xres_fm_pl_gelu_kernel(
         for a in range(PASSES - 1):
             whole = sb.tile([P, PACK, T], F32, name=f"raw{a}")
             nc.sync.dma_start(out=whole[:], in_=xr_rows[a])
+            if a == 0:
+                nc.sync.dma_start(out=bias_row[0:P:32, :], in_=b.rearrange("(q n) -> q n", n=P))
             for h in range(2):
                 raw[a, h] = whole[:, :, h * HALF : (h + 1) * HALF]
-        nc.sync.dma_start(out=bias[:], in_=b.rearrange("(p r) -> p r", r=PACK))
         nc.sync.dma_start(out=x4_last[0][:].bitcast(I32), in_=x4_rows[:, 3, :QUARTER])
         for h in range(2):
             part = sb.tile([P, PACK, HALF], F32, name=f"raw_last{h}")
@@ -148,7 +152,7 @@ def tile_mix_xres_fm_pl_gelu_kernel(
 
         def activate(h, r, lo, hi):
             nc.scalar.activation(
-                out=result[h][:, r, lo:hi], in_=acc[h, r][:, lo:hi], func=GELU, bias=bias[:, r : r + 1]
+                out=result[h][:, r, lo:hi], in_=acc[h, r][:, lo:hi], func=GELU, bias=bias[:, 32 * r : 32 * r + 1]
             )
 
         def round_result(copy, h, lo, hi):
@@ -165,8 +169,9 @@ def tile_mix_xres_fm_pl_gelu_kernel(
         vec, act = nc.vector.tensor_copy, nc.scalar.copy
         multiply_x4(0, 0)
         multiply_x4(0, 1)
-        for a in (1, 2):
-            multiply_x4(a, 0)
+        multiply_x4(1, 0)
+        multiply_x4(1, 1)
+        multiply_x4(2, 0)
         for a in range(PASSES - 1):
             group_shared((a, 0))
             group_shared((a, 1))
@@ -176,16 +181,23 @@ def tile_mix_xres_fm_pl_gelu_kernel(
                 multiply_x4(3, 0)
             multiply_xr(a, 0)
             multiply_xr(a, 1)
-            if a < 2:
-                multiply_x4(a + 1, 1)
+            if a == 0:
+                multiply_x4(2, 1)
+                nc.vector.tensor_copy(
+                    out=bias_dealt[:].rearrange("p (r i) -> p r i", r=PACK),
+                    in_=bias_row[:].rearrange("p (i r) -> p r i", r=PACK),
+                )
+                nc.vector.transpose(out=bias[:], in_=bias_dealt[:])
         group(act, (3, 0), HALF - 192, HALF)
         group(vec, (3, 0), 0, QUARTER)
         group(vec, (3, 0), QUARTER, HALF - 192)
         quantize((3, 0), 0, QUARTER)
         quantize((3, 0), QUARTER, HALF)
         multiply_xr(3, 0)
-        for r in range(PACK):
+        for r in range(PACK - 1):
             activate(0, r, 0, HALF)
+        activate(0, PACK - 1, 0, QUARTER)
+        activate(0, PACK - 1, QUARTER, HALF)
         group(vec, (3, 1), 0, QUARTER)
         group(vec, (3, 1), QUARTER, HALF)
         quantize((3, 1), 0, QUARTER)

@@ -22,6 +22,7 @@ HALF = 512
 QUARTER = 256
 SCALAR_COLS = 224
 LAST = 384
+ALIGN = 256
 
 
 def interleave(copy, dst, src):
@@ -40,29 +41,29 @@ def tile_mix_xres_fm_pl_gelu_kernel(
         ps = ctx.enter_context(tc.psum_pool(name="ps", bufs=1))
         ctx.enter_context(tc.manual_schedule())
 
-        w_raw = sb.tile([P, PASSES, 2 * M], U8, align_bytes=64)
-        ws_raw = sb.tile([P, PASSES, M], U8, align_bytes=64)
-        w_codes = [sb.tile([P, 2 * M], U8, align_bytes=64, name=f"w_codes{a}") for a in range(PASSES)]
-        w_scales = [sb.tile([P, M], U8, align_bytes=64, name=f"w_scales{a}") for a in range(PASSES)]
-        x4_codes = sb.tile([P, PASSES - 1, 2 * T], U8, align_bytes=64)
-        x4_last = [sb.tile([P, 2 * HALF], U8, align_bytes=64, name=f"x4_last{h}") for h in range(2)]
-        x4_planes = sb.tile([P, PASSES, T], U8, align_bytes=64)
-        bias_row = sb.tile([P, P], F32, align_bytes=64)
-        bias_dealt = sb.tile([P, P], F32, align_bytes=64)
-        bias = sb.tile([P, P], F32, align_bytes=64)
+        w_raw = sb.tile([P, PASSES, 2 * M], U8, align_bytes=ALIGN)
+        ws_raw = sb.tile([P, PASSES, M], U8, align_bytes=ALIGN)
+        w_codes = [sb.tile([P, 2 * M], U8, align_bytes=ALIGN, name=f"w_codes{a}") for a in range(PASSES)]
+        w_scales = [sb.tile([P, M], U8, align_bytes=ALIGN, name=f"w_scales{a}") for a in range(PASSES)]
+        x4_codes = sb.tile([P, PASSES - 1, 2 * T], U8, align_bytes=ALIGN)
+        x4_last = [sb.tile([P, 2 * HALF], U8, align_bytes=ALIGN, name=f"x4_last{h}") for h in range(2)]
+        x4_planes = sb.tile([P, PASSES, T], U8, align_bytes=ALIGN)
+        bias_row = sb.tile([P, P], F32, align_bytes=ALIGN)
+        bias_dealt = sb.tile([P, P], F32, align_bytes=ALIGN)
+        bias = sb.tile([P, P], F32, align_bytes=ALIGN)
         pieces = [(a, h) for a in range(PASSES) for h in range(2)]
-        grouped = {k: sb.tile([P, HALF, PACK], BF16, align_bytes=64, name=f"grouped{k[0]}{k[1]}") for k in pieces}
-        xr_codes = {k: sb.tile([P, HALF], U32, align_bytes=64, name=f"xr_codes{k[0]}{k[1]}") for k in pieces}
-        xr_scales = {k: sb.tile([P, HALF], U8, align_bytes=64, name=f"xr_scales{k[0]}{k[1]}") for k in pieces}
+        grouped = {k: sb.tile([P, HALF, PACK], BF16, align_bytes=ALIGN, name=f"grouped{k[0]}{k[1]}") for k in pieces}
+        xr_codes = {k: sb.tile([P, HALF], U32, align_bytes=ALIGN, name=f"xr_codes{k[0]}{k[1]}") for k in pieces}
+        xr_scales = {k: sb.tile([P, HALF], U8, align_bytes=ALIGN, name=f"xr_scales{k[0]}{k[1]}") for k in pieces}
         acc = {
             (h, r): ps.tile([P, HALF], F32, name=f"acc{h}{r}") for h in range(2) for r in range(PACK)
         }
-        result = [sb.tile([P, PACK, HALF], F32, name=f"result{h}") for h in range(2)]
-        rounded = [sb.tile([P, HALF, PACK], BF16, align_bytes=64, name=f"rounded{h}") for h in range(2)]
-        out_codes = sb.tile([P, T], U32, align_bytes=64)
-        out_scales = sb.tile([P, T], U8, align_bytes=64)
+        result = [sb.tile([P, PACK, HALF], F32, align_bytes=ALIGN, name=f"result{h}") for h in range(2)]
+        rounded = [sb.tile([P, HALF, PACK], BF16, align_bytes=ALIGN, name=f"rounded{h}") for h in range(2)]
+        out_codes = sb.tile([P, T], U32, align_bytes=ALIGN)
+        out_scales = sb.tile([P, T], U8, align_bytes=ALIGN)
 
-        warm = sb.tile([P, 8], F32)
+        warm = sb.tile([P, 8], F32, align_bytes=ALIGN)
         nc.gpsimd.memset(warm[:], 0.0)
         nc.scalar.activation(out=warm[:, 4:5], in_=warm[:, 0:1], func=GELU)
         nc.vector.memset(ws_raw[:].bitcast(I32), 0)
@@ -87,7 +88,7 @@ def tile_mix_xres_fm_pl_gelu_kernel(
         xr_rows = xr.rearrange("(a p j) t -> a p j t", p=P, j=PACK)
         raw = {}
         for a in range(PASSES - 1):
-            whole = sb.tile([P, PACK, T], F32, name=f"raw{a}")
+            whole = sb.tile([P, PACK, T], F32, align_bytes=ALIGN, name=f"raw{a}")
             nc.sync.dma_start(out=whole[:], in_=xr_rows[a])
             if a == 0:
                 nc.sync.dma_start(out=bias_row[0:P:32, :], in_=b.rearrange("(q n) -> q n", n=P))
@@ -95,7 +96,7 @@ def tile_mix_xres_fm_pl_gelu_kernel(
                 raw[a, h] = whole[:, :, h * HALF : (h + 1) * HALF]
         nc.sync.dma_start(out=x4_last[0][:].bitcast(I32), in_=x4_rows[:, 3, :QUARTER])
         for h in range(2):
-            part = sb.tile([P, PACK, HALF], F32, name=f"raw_last{h}")
+            part = sb.tile([P, PACK, HALF], F32, align_bytes=ALIGN, name=f"raw_last{h}")
             nc.sync.dma_start(out=part[:], in_=xr_rows[PASSES - 1][:, :, h * HALF : (h + 1) * HALF])
             raw[PASSES - 1, h] = part[:]
         nc.sync.dma_start(out=x4_last[1][:].bitcast(I32), in_=x4_rows[:, 3, QUARTER:])
@@ -172,13 +173,11 @@ def tile_mix_xres_fm_pl_gelu_kernel(
         multiply_x4(1, 0)
         multiply_x4(1, 1)
         multiply_x4(2, 0)
-        for a in range(PASSES - 1):
+        for a in range(PASSES - 2):
             group_shared((a, 0))
             group_shared((a, 1))
             quantize((a, 0))
             quantize((a, 1))
-            if a == 2:
-                multiply_x4(3, 0)
             multiply_xr(a, 0)
             multiply_xr(a, 1)
             if a == 0:
@@ -188,6 +187,17 @@ def tile_mix_xres_fm_pl_gelu_kernel(
                     in_=bias_row[:].rearrange("p (i r) -> p r i", r=PACK),
                 )
                 nc.vector.transpose(out=bias[:], in_=bias_dealt[:])
+        group(act, (2, 0), 0, 160)
+        group(vec, (2, 0), 160, HALF)
+        group(act, (2, 1), 0, QUARTER)
+        group(vec, (2, 1), QUARTER, LAST)
+        quantize((2, 0))
+        group(vec, (2, 1), LAST, HALF)
+        quantize((2, 1), 0, QUARTER)
+        quantize((2, 1), QUARTER, HALF)
+        multiply_x4(3, 0)
+        multiply_xr(2, 0)
+        multiply_xr(2, 1)
         group(act, (3, 0), HALF - 192, HALF)
         group(vec, (3, 0), 0, QUARTER)
         group(vec, (3, 0), QUARTER, HALF - 192)

@@ -227,7 +227,8 @@ def tile_mix_xres_fm_pl_gelu_kernel(
         round_result(vec, 1, QUARTER, LAST)
         round_result(act, 1, LAST, HALF)
         quantize_result(1, 0, QUARTER)
-        quantize_result(1, QUARTER, HALF)
+        quantize_result(1, QUARTER, LAST)
+        quantize_result(1, LAST, HALF)
 
         rows = out_0.rearrange("(p r) t -> p r t", r=PACK)
         words = out_1[0].rearrange("p t i -> p (t i)").bitcast(I32)
@@ -237,7 +238,7 @@ def tile_mix_xres_fm_pl_gelu_kernel(
             nc.sync.dma_start(out=rows[:, r, HALF:], in_=result[1][:, r, :])
         nc.sync.dma_start(out=words[:, :HALF], in_=out_codes[:, :HALF].bitcast(I32))
         nc.sync.dma_start(out=rows[:, 2:, HALF:], in_=result[1][:, 2:, :])
-        for lo, hi in ((HALF, HALF + QUARTER), (HALF + QUARTER, T)):
+        for lo, hi in ((HALF, HALF + LAST), (HALF + LAST, T)):
             nc.sync.dma_start(out=words[:, lo:hi], in_=out_codes[:, lo:hi].bitcast(I32))
         for r in range(4):
             queue = nc.sync if r == 0 else nc.scalar

@@ -27,8 +27,8 @@ ALIGN = 256
 
 def interleave(copy, dst, src):
     copy(
-        out=dst.rearrange("p (c i) j -> p c j i", i=4),
-        in_=src.rearrange("p j (c i) -> p c j i", i=4),
+        out=dst.rearrange("p (c i) j -> p c j i", i=8),
+        in_=src.rearrange("p j (c i) -> p c j i", i=8),
     )
 
 

@@ -151,6 +151,24 @@ def tile_mix_xres_fm_pl_gelu_kernel(
         def multiply_xr(a, h):
             multiply(h, a, xr_codes[a, h][:].bitcast(FP8X4), xr_scales[a, h][:], False, a == PASSES - 1)
 
+        def one_pass(h, r, lo, hi, stop):
+            a = PASSES - 1
+            nc.tensor.matmul_mx(
+                out=acc[h, r][:, lo:hi],
+                lhsT=w_codes[a][:, 2 * P * r : 2 * P * (r + 1)].bitcast(FP4X4),
+                lhsT_scale=w_scales[a][:, P * r : P * (r + 1)],
+                rhs=xr_codes[a, h][:, lo:hi].bitcast(FP8X4),
+                rhs_scale=xr_scales[a, h][:, lo:hi],
+                start=False,
+                stop=stop,
+            )
+
+        def close(h):
+            for lo, hi in ((0, QUARTER), (QUARTER, LAST), (LAST, HALF)):
+                one_pass(h, 0, lo, hi, hi == HALF)
+            for r in range(1, PACK):
+                one_pass(h, r, 0, HALF, True)
+
         def activate(h, r, lo, hi):
             nc.scalar.activation(
                 out=result[h][:, r, lo:hi], in_=acc[h, r][:, lo:hi], func=GELU, bias=bias[:, 32 * r : 32 * r + 1]
@@ -202,8 +220,9 @@ def tile_mix_xres_fm_pl_gelu_kernel(
         group(vec, (3, 0), 0, QUARTER)
         group(vec, (3, 0), QUARTER, HALF - 192)
         quantize((3, 0), 0, QUARTER)
-        quantize((3, 0), QUARTER, HALF)
-        multiply_xr(3, 0)
+        quantize((3, 0), QUARTER, LAST)
+        quantize((3, 0), LAST, HALF)
+        close(0)
         for r in range(PACK - 1):
             activate(0, r, 0, HALF)
         activate(0, PACK - 1, 0, QUARTER)
@@ -211,13 +230,14 @@ def tile_mix_xres_fm_pl_gelu_kernel(
         group(vec, (3, 1), 0, QUARTER)
         group(vec, (3, 1), QUARTER, HALF)
         quantize((3, 1), 0, QUARTER)
-        quantize((3, 1), QUARTER, HALF)
+        quantize((3, 1), QUARTER, LAST)
+        quantize((3, 1), LAST, HALF)
         round_result(vec, 0, 0, QUARTER)
         round_result(vec, 0, QUARTER, HALF)
         quantize_result(0, 0, QUARTER)
         quantize_result(0, QUARTER, HALF)
         multiply_x4(3, 1)
-        multiply_xr(3, 1)
+        close(1)
         activate(1, 0, 0, HALF)
         activate(1, 1, 0, HALF)
         for lo, hi in ((0, QUARTER), (QUARTER, LAST), (LAST, HALF)):

@@ -23,6 +23,7 @@ QUARTER = 256
 SCALAR_COLS = 224
 LAST = 384
 ALIGN = 256
+DMA_ALIGN = 2048
 
 
 def interleave(copy, dst, src):
@@ -41,14 +42,14 @@ def tile_mix_xres_fm_pl_gelu_kernel(
         ps = ctx.enter_context(tc.psum_pool(name="ps", bufs=1))
         ctx.enter_context(tc.manual_schedule())
 
-        w_raw = sb.tile([P, PASSES, 2 * M], U8, align_bytes=ALIGN)
-        ws_raw = sb.tile([P, PASSES, M], U8, align_bytes=ALIGN)
+        w_raw = sb.tile([P, PASSES, 2 * M], U8, align_bytes=DMA_ALIGN)
+        ws_raw = sb.tile([P, PASSES, M], U8, align_bytes=DMA_ALIGN)
         w_codes = [sb.tile([P, 2 * M], U8, align_bytes=ALIGN, name=f"w_codes{a}") for a in range(PASSES)]
         w_scales = [sb.tile([P, M], U8, align_bytes=ALIGN, name=f"w_scales{a}") for a in range(PASSES)]
-        x4_codes = sb.tile([P, PASSES - 1, 2 * T], U8, align_bytes=ALIGN)
-        x4_last = [sb.tile([P, 2 * HALF], U8, align_bytes=ALIGN, name=f"x4_last{h}") for h in range(2)]
-        x4_planes = sb.tile([P, PASSES, T], U8, align_bytes=ALIGN)
-        bias_row = sb.tile([P, P], F32, align_bytes=ALIGN)
+        x4_codes = sb.tile([P, PASSES - 1, 2 * T], U8, align_bytes=DMA_ALIGN)
+        x4_last = [sb.tile([P, 2 * HALF], U8, align_bytes=DMA_ALIGN, name=f"x4_last{h}") for h in range(2)]
+        x4_planes = sb.tile([P, PASSES, T], U8, align_bytes=DMA_ALIGN)
+        bias_row = sb.tile([P, P], F32, align_bytes=DMA_ALIGN)
         bias_dealt = sb.tile([P, P], F32, align_bytes=ALIGN)
         bias = sb.tile([P, P], F32, align_bytes=ALIGN)
         pieces = [(a, h) for a in range(PASSES) for h in range(2)]
@@ -58,10 +59,10 @@ def tile_mix_xres_fm_pl_gelu_kernel(
         acc = {
             (h, r): ps.tile([P, HALF], F32, name=f"acc{h}{r}") for h in range(2) for r in range(PACK)
         }
-        result = [sb.tile([P, PACK, HALF], F32, align_bytes=ALIGN, name=f"result{h}") for h in range(2)]
+        result = [sb.tile([P, PACK, HALF], F32, align_bytes=DMA_ALIGN, name=f"result{h}") for h in range(2)]
         rounded = [sb.tile([P, HALF, PACK], BF16, align_bytes=ALIGN, name=f"rounded{h}") for h in range(2)]
-        out_codes = sb.tile([P, T], U32, align_bytes=ALIGN)
-        out_scales = sb.tile([P, T], U8, align_bytes=ALIGN)
+        out_codes = sb.tile([P, T], U32, align_bytes=DMA_ALIGN)
+        out_scales = sb.tile([P, T], U8, align_bytes=DMA_ALIGN)
 
         warm = sb.tile([P, 8], F32, align_bytes=ALIGN)
         nc.gpsimd.memset(warm[:], 0.0)
@@ -88,7 +89,7 @@ def tile_mix_xres_fm_pl_gelu_kernel(
         xr_rows = xr.rearrange("(a p j) t -> a p j t", p=P, j=PACK)
         raw = {}
         for a in range(PASSES - 1):
-            whole = sb.tile([P, PACK, T], F32, align_bytes=ALIGN, name=f"raw{a}")
+            whole = sb.tile([P, PACK, T], F32, align_bytes=DMA_ALIGN, name=f"raw{a}")
             nc.sync.dma_start(out=whole[:], in_=xr_rows[a])
             if a == 0:
                 nc.sync.dma_start(out=bias_row[0:P:32, :], in_=b.rearrange("(q n) -> q n", n=P))
@@ -96,7 +97,7 @@ def tile_mix_xres_fm_pl_gelu_kernel(
                 raw[a, h] = whole[:, :, h * HALF : (h + 1) * HALF]
         nc.sync.dma_start(out=x4_last[0][:].bitcast(I32), in_=x4_rows[:, 3, :QUARTER])
         for h in range(2):
-            part = sb.tile([P, PACK, HALF], F32, align_bytes=ALIGN, name=f"raw_last{h}")
+            part = sb.tile([P, PACK, HALF], F32, align_bytes=DMA_ALIGN, name=f"raw_last{h}")
             nc.sync.dma_start(out=part[:], in_=xr_rows[PASSES - 1][:, :, h * HALF : (h + 1) * HALF])
             raw[PASSES - 1, h] = part[:]
         nc.sync.dma_start(out=x4_last[1][:].bitcast(I32), in_=x4_rows[:, 3, QUARTER:])

@@ -23,7 +23,6 @@ QUARTER = 256
 SCALAR_COLS = 224
 LAST = 384
 ALIGN = 256
-DMA_ALIGN = 2048
 
 
 def interleave(copy, dst, src):
@@ -42,74 +41,77 @@ def tile_mix_xres_fm_pl_gelu_kernel(
         ps = ctx.enter_context(tc.psum_pool(name="ps", bufs=1))
         ctx.enter_context(tc.manual_schedule())
 
-        w_raw = sb.tile([P, PASSES, 2 * M], U8, align_bytes=DMA_ALIGN)
-        ws_raw = sb.tile([P, PASSES, M], U8, align_bytes=DMA_ALIGN)
-        w_codes = [sb.tile([P, 2 * M], U8, align_bytes=ALIGN, name=f"w_codes{a}") for a in range(PASSES)]
-        w_scales = [sb.tile([P, M], U8, align_bytes=ALIGN, name=f"w_scales{a}") for a in range(PASSES)]
-        x4_codes = sb.tile([P, PASSES - 1, 2 * T], U8, align_bytes=DMA_ALIGN)
-        x4_last = [sb.tile([P, 2 * HALF], U8, align_bytes=DMA_ALIGN, name=f"x4_last{h}") for h in range(2)]
-        x4_planes = sb.tile([P, PASSES, T], U8, align_bytes=DMA_ALIGN)
-        bias_row = sb.tile([P, P], F32, align_bytes=DMA_ALIGN)
-        bias_dealt = sb.tile([P, P], F32, align_bytes=ALIGN)
-        bias = sb.tile([P, P], F32, align_bytes=ALIGN)
-        pieces = [(a, h) for a in range(PASSES) for h in range(2)]
-        grouped = {k: sb.tile([P, HALF, PACK], BF16, align_bytes=ALIGN, name=f"grouped{k[0]}{k[1]}") for k in pieces}
-        xr_codes = {k: sb.tile([P, HALF], U32, align_bytes=ALIGN, name=f"xr_codes{k[0]}{k[1]}") for k in pieces}
-        xr_scales = {k: sb.tile([P, HALF], U8, align_bytes=ALIGN, name=f"xr_scales{k[0]}{k[1]}") for k in pieces}
-        acc = {
-            (h, r): ps.tile([P, HALF], F32, name=f"acc{h}{r}") for h in range(2) for r in range(PACK)
-        }
-        result = [sb.tile([P, PACK, HALF], F32, align_bytes=DMA_ALIGN, name=f"result{h}") for h in range(2)]
-        rounded = [sb.tile([P, HALF, PACK], BF16, align_bytes=ALIGN, name=f"rounded{h}") for h in range(2)]
-        out_codes = sb.tile([P, T], U32, align_bytes=DMA_ALIGN)
-        out_scales = sb.tile([P, T], U8, align_bytes=DMA_ALIGN)
+        def tile(shape, dtype, name):
+            return sb.tile(shape, dtype, align_bytes=ALIGN, name=name)
 
-        warm = sb.tile([P, 8], F32, align_bytes=ALIGN)
+        w_raw = [tile([P, 2, 2 * M], U8, f"w_raw{c}") for c in range(2)]
+        ws_raw = tile([P, PASSES, M], U8, "ws_raw")
+        w_codes = [tile([P, 2 * M], U8, f"w_codes{a}") for a in range(PASSES)]
+        w_planes = [tile([P, M], U8, f"w_planes{a}") for a in range(PASSES)]
+        x4_codes = [tile([P, 2 * T], U8, f"x4_codes{a}") for a in range(PASSES - 1)]
+        x4_last = [tile([P, 2 * HALF], U8, f"x4_last{h}") for h in range(2)]
+        x4_planes = tile([P, PASSES, T], U8, "x4_planes")
+        bias_row = tile([P, P], F32, "bias_row")
+        bias_dealt = tile([P, P], F32, "bias_dealt")
+        bias = tile([P, P], F32, "bias")
+        pieces = [(a, h) for a in range(PASSES) for h in range(2)]
+        grouped = {k: tile([P, HALF, PACK], BF16, f"grouped{k[0]}{k[1]}") for k in pieces}
+        xr_codes = {k: tile([P, HALF], U32, f"xr_codes{k[0]}{k[1]}") for k in pieces}
+        xr_scales = {k: tile([P, HALF], U8, f"xr_scales{k[0]}{k[1]}") for k in pieces}
+        acc = {(h, r): ps.tile([P, HALF], F32, name=f"acc{h}{r}") for h in range(2) for r in range(PACK)}
+        result = [tile([P, PACK, HALF], F32, f"result{h}") for h in range(2)]
+        rounded = [tile([P, HALF, PACK], BF16, f"rounded{h}") for h in range(2)]
+        out_codes = tile([P, T], U32, "out_codes")
+        out_scales = tile([P, T], U8, "out_scales")
+
+        warm = tile([P, 8], F32, "warm")
         nc.gpsimd.memset(warm[:], 0.0)
         nc.scalar.activation(out=warm[:, 4:5], in_=warm[:, 0:1], func=GELU)
         nc.vector.memset(ws_raw[:].bitcast(I32), 0)
         nc.vector.memset(x4_planes[:].bitcast(I32), 0)
         nc.vector.memset(bias_row[:], 0.0)
 
-        nc.sync.dma_start(out=w_raw[:].bitcast(I32), in_=w4_words.rearrange("a p n -> p a n").bitcast(I32))
-
-        def load_scale_rows(plane, scales, r):
-            nc.sync.dma_start(
-                out=plane[r:P:32].bitcast(I32),
-                in_=scales.rearrange("a (q r) n -> r q a n", r=4)[r].bitcast(I32),
-            )
-
-        for r in range(4):
-            load_scale_rows(ws_raw, w4_scales, r)
+        w_rows = w4_words.rearrange("a p n -> p a n").bitcast(I32)
         x4_rows = x4_words.rearrange("a p n -> p a n").bitcast(I32)
-        nc.sync.dma_start(out=x4_codes[:, :2, :].bitcast(I32), in_=x4_rows[:, :2, :])
-        for r in range(4):
-            load_scale_rows(x4_planes, x4_scales, r)
-        nc.sync.dma_start(out=x4_codes[:, 2:3, :].bitcast(I32), in_=x4_rows[:, 2:3, :])
         xr_rows = xr.rearrange("(a p j) t -> a p j t", p=P, j=PACK)
+
+        def load_planes(plane, scales):
+            for r in range(4):
+                nc.sync.dma_start(
+                    out=plane[r:P:32].bitcast(I32),
+                    in_=scales.rearrange("a (q r) n -> r q a n", r=4)[r].bitcast(I32),
+                )
+
+        nc.sync.dma_start(out=w_raw[0][:].bitcast(I32), in_=w_rows[:, :2, :])
+        load_planes(ws_raw, w4_scales)
+        nc.sync.dma_start(out=w_raw[1][:].bitcast(I32), in_=w_rows[:, 2:, :])
+        for a in range(2):
+            nc.sync.dma_start(out=x4_codes[a][:].bitcast(I32), in_=x4_rows[:, a, :])
+        load_planes(x4_planes, x4_scales)
+        nc.sync.dma_start(out=bias_row[0:P:32, :], in_=b.rearrange("(q n) -> q n", n=P))
+        nc.sync.dma_start(out=x4_codes[2][:].bitcast(I32), in_=x4_rows[:, 2, :])
         raw = {}
         for a in range(PASSES - 1):
-            whole = sb.tile([P, PACK, T], F32, align_bytes=DMA_ALIGN, name=f"raw{a}")
+            whole = tile([P, PACK, T], F32, f"raw{a}")
             nc.sync.dma_start(out=whole[:], in_=xr_rows[a])
-            if a == 0:
-                nc.sync.dma_start(out=bias_row[0:P:32, :], in_=b.rearrange("(q n) -> q n", n=P))
             for h in range(2):
                 raw[a, h] = whole[:, :, h * HALF : (h + 1) * HALF]
         nc.sync.dma_start(out=x4_last[0][:].bitcast(I32), in_=x4_rows[:, 3, :QUARTER])
         for h in range(2):
-            part = sb.tile([P, PACK, HALF], F32, align_bytes=DMA_ALIGN, name=f"raw_last{h}")
+            part = tile([P, PACK, HALF], F32, f"raw_last{h}")
             nc.sync.dma_start(out=part[:], in_=xr_rows[PASSES - 1][:, :, h * HALF : (h + 1) * HALF])
             raw[PASSES - 1, h] = part[:]
         nc.sync.dma_start(out=x4_last[1][:].bitcast(I32), in_=x4_rows[:, 3, QUARTER:])
 
         for a in range(PASSES):
             nc.vector.tensor_copy(
-                out=w_codes[a][:].bitcast(U16).rearrange("p (r m) -> p r m", r=PACK),
-                in_=w_raw[:, a, :].bitcast(U16).rearrange("p (m r) -> p r m", r=PACK),
-            )
-            nc.vector.tensor_copy(
-                out=w_scales[a][:].rearrange("p (r m) -> p r m", r=PACK),
+                out=w_planes[a][:].rearrange("p (r m) -> p r m", r=PACK),
                 in_=ws_raw[:, a, :].rearrange("p (m r) -> p r m", r=PACK),
+            )
+        for a in range(PASSES):
+            nc.vector.tensor_copy(
+                out=w_codes[a][:].bitcast(U16).rearrange("p (r m) -> p r m", r=PACK),
+                in_=w_raw[a // 2][:, a % 2, :].bitcast(U16).rearrange("p (m r) -> p r m", r=PACK),
             )
 
         def group(copy, piece, lo, hi):
@@ -126,49 +128,38 @@ def tile_mix_xres_fm_pl_gelu_kernel(
                 in_=grouped[piece][:, lo:hi, :].rearrange("p t j -> p (t j)"),
             )
 
-        def multiply(h, a, rhs, rhs_scale, start, stop):
-            for r in range(PACK):
-                nc.tensor.matmul_mx(
-                    out=acc[h, r][:],
-                    lhsT=w_codes[a][:, 2 * P * r : 2 * P * (r + 1)].bitcast(FP4X4),
-                    lhsT_scale=w_scales[a][:, P * r : P * (r + 1)],
-                    rhs=rhs,
-                    rhs_scale=rhs_scale,
-                    start=start,
-                    stop=stop,
-                )
-
-        def multiply_x4(a, h):
-            codes = x4_last[h][:] if a == PASSES - 1 else x4_codes[:, a, 2 * HALF * h : 2 * HALF * (h + 1)]
-            multiply(
-                h,
-                a,
-                codes.bitcast(FP4X4),
-                x4_planes[:, a, HALF * h : HALF * (h + 1)],
-                a == 0,
-                False,
-            )
-
-        def multiply_xr(a, h):
-            multiply(h, a, xr_codes[a, h][:].bitcast(FP8X4), xr_scales[a, h][:], False, a == PASSES - 1)
-
-        def one_pass(h, r, lo, hi, stop):
-            a = PASSES - 1
+        def one_pass(out, a, r, rhs, rhs_scale, start, stop):
             nc.tensor.matmul_mx(
-                out=acc[h, r][:, lo:hi],
+                out=out,
                 lhsT=w_codes[a][:, 2 * P * r : 2 * P * (r + 1)].bitcast(FP4X4),
-                lhsT_scale=w_scales[a][:, P * r : P * (r + 1)],
-                rhs=xr_codes[a, h][:, lo:hi].bitcast(FP8X4),
-                rhs_scale=xr_scales[a, h][:, lo:hi],
-                start=False,
+                lhsT_scale=w_planes[a][:, P * r : P * (r + 1)],
+                rhs=rhs,
+                rhs_scale=rhs_scale,
+                start=start,
                 stop=stop,
             )
 
+        def multiply_x4(a, h):
+            codes = x4_last[h][:] if a == PASSES - 1 else x4_codes[a][:, 2 * HALF * h : 2 * HALF * (h + 1)]
+            for r in range(PACK):
+                one_pass(
+                    acc[h, r][:], a, r, codes.bitcast(FP4X4), x4_planes[:, a, HALF * h : HALF * (h + 1)], a == 0, False
+                )
+
+        def xr_pass(a, h, r, lo, hi, stop):
+            one_pass(
+                acc[h, r][:, lo:hi], a, r, xr_codes[a, h][:, lo:hi].bitcast(FP8X4), xr_scales[a, h][:, lo:hi], False, stop
+            )
+
+        def multiply_xr(a, h):
+            for r in range(PACK):
+                xr_pass(a, h, r, 0, HALF, False)
+
         def close(h):
             for lo, hi in ((0, QUARTER), (QUARTER, LAST), (LAST, HALF)):
-                one_pass(h, 0, lo, hi, hi == HALF)
+                xr_pass(PASSES - 1, h, 0, lo, hi, hi == HALF)
             for r in range(1, PACK):
-                one_pass(h, r, 0, HALF, True)
+                xr_pass(PASSES - 1, h, r, 0, HALF, True)
 
         def activate(h, r, lo, hi):
             nc.scalar.activation(

@@ -44,11 +44,11 @@ def tile_mix_xres_fm_pl_gelu_kernel(
         def tile(shape, dtype, name):
             return sb.tile(shape, dtype, align_bytes=ALIGN, name=name)
 
-        w_raw = [tile([P, 2, 2 * M], U8, f"w_raw{c}") for c in range(2)]
+        w_raw = tile([P, PASSES, 2 * M], U8, "w_raw")
         ws_raw = tile([P, PASSES, M], U8, "ws_raw")
         w_codes = [tile([P, 2 * M], U8, f"w_codes{a}") for a in range(PASSES)]
         w_planes = [tile([P, M], U8, f"w_planes{a}") for a in range(PASSES)]
-        x4_codes = [tile([P, 2 * T], U8, f"x4_codes{a}") for a in range(PASSES - 1)]
+        x4_codes = tile([P, PASSES - 1, 2 * T], U8, "x4_codes")
         x4_last = [tile([P, 2 * HALF], U8, f"x4_last{h}") for h in range(2)]
         x4_planes = tile([P, PASSES, T], U8, "x4_planes")
         bias_row = tile([P, P], F32, "bias_row")
@@ -82,40 +82,41 @@ def tile_mix_xres_fm_pl_gelu_kernel(
                     in_=scales.rearrange("a (q r) n -> r q a n", r=4)[r].bitcast(I32),
                 )
 
-        nc.sync.dma_start(out=w_raw[0][:].bitcast(I32), in_=w_rows[:, :2, :])
+        nc.sync.dma_start(out=w_raw[:].bitcast(I32), in_=w_rows)
         load_planes(ws_raw, w4_scales)
-        nc.sync.dma_start(out=w_raw[1][:].bitcast(I32), in_=w_rows[:, 2:, :])
-        for a in range(2):
-            nc.sync.dma_start(out=x4_codes[a][:].bitcast(I32), in_=x4_rows[:, a, :])
+        nc.sync.dma_start(out=x4_codes[:, :2, :].bitcast(I32), in_=x4_rows[:, :2, :])
         load_planes(x4_planes, x4_scales)
-        nc.sync.dma_start(out=bias_row[0:P:32, :], in_=b.rearrange("(q n) -> q n", n=P))
-        nc.sync.dma_start(out=x4_codes[2][:].bitcast(I32), in_=x4_rows[:, 2, :])
-        raw = {}
+        nc.sync.dma_start(out=x4_codes[:, 2:3, :].bitcast(I32), in_=x4_rows[:, 2:3, :])
+        raw = []
         for a in range(PASSES - 1):
-            whole = tile([P, PACK, T], F32, f"raw{a}")
-            nc.sync.dma_start(out=whole[:], in_=xr_rows[a])
-            for h in range(2):
-                raw[a, h] = whole[:, :, h * HALF : (h + 1) * HALF]
+            raw.append(tile([P, PACK, T], F32, f"raw{a}"))
+            nc.sync.dma_start(out=raw[a][:], in_=xr_rows[a])
+            if a == 0:
+                nc.sync.dma_start(out=bias_row[0:P:32, :], in_=b.rearrange("(q n) -> q n", n=P))
         nc.sync.dma_start(out=x4_last[0][:].bitcast(I32), in_=x4_rows[:, 3, :QUARTER])
-        for h in range(2):
-            part = tile([P, PACK, HALF], F32, f"raw_last{h}")
-            nc.sync.dma_start(out=part[:], in_=xr_rows[PASSES - 1][:, :, h * HALF : (h + 1) * HALF])
-            raw[PASSES - 1, h] = part[:]
+        raw_last = []
+        for c in range(T // QUARTER):
+            raw_last.append(tile([P, PACK, QUARTER], F32, f"raw_last{c}"))
+            nc.sync.dma_start(out=raw_last[c][:], in_=xr_rows[PASSES - 1][:, :, c * QUARTER : (c + 1) * QUARTER])
         nc.sync.dma_start(out=x4_last[1][:].bitcast(I32), in_=x4_rows[:, 3, QUARTER:])
 
         for a in range(PASSES):
             nc.vector.tensor_copy(
+                out=w_codes[a][:].bitcast(U16).rearrange("p (r m) -> p r m", r=PACK),
+                in_=w_raw[:, a, :].bitcast(U16).rearrange("p (m r) -> p r m", r=PACK),
+            )
+            nc.vector.tensor_copy(
                 out=w_planes[a][:].rearrange("p (r m) -> p r m", r=PACK),
                 in_=ws_raw[:, a, :].rearrange("p (m r) -> p r m", r=PACK),
             )
-        for a in range(PASSES):
-            nc.vector.tensor_copy(
-                out=w_codes[a][:].bitcast(U16).rearrange("p (r m) -> p r m", r=PACK),
-                in_=w_raw[a // 2][:, a % 2, :].bitcast(U16).rearrange("p (m r) -> p r m", r=PACK),
-            )
 
         def group(copy, piece, lo, hi):
-            interleave(copy, grouped[piece][:, lo:hi, :], raw[piece][:, :, lo:hi])
+            a, h = piece
+            if a < PASSES - 1:
+                src = raw[a][:, :, h * HALF + lo : h * HALF + hi]
+            else:
+                src = raw_last[2 * h + lo // QUARTER][:, :, lo % QUARTER : (hi - 1) % QUARTER + 1]
+            interleave(copy, grouped[piece][:, lo:hi, :], src)
 
         def group_shared(piece):
             group(nc.scalar.copy, piece, 0, SCALAR_COLS)
@@ -139,9 +140,9 @@ def tile_mix_xres_fm_pl_gelu_kernel(
                 stop=stop,
             )
 
-        def multiply_x4(a, h):
-            codes = x4_last[h][:] if a == PASSES - 1 else x4_codes[a][:, 2 * HALF * h : 2 * HALF * (h + 1)]
-            for r in range(PACK):
+        def multiply_x4(a, h, rows=range(PACK)):
+            codes = x4_last[h][:] if a == PASSES - 1 else x4_codes[:, a, 2 * HALF * h : 2 * HALF * (h + 1)]
+            for r in rows:
                 one_pass(
                     acc[h, r][:], a, r, codes.bitcast(FP4X4), x4_planes[:, a, HALF * h : HALF * (h + 1)], a == 0, False
                 )
@@ -155,11 +156,16 @@ def tile_mix_xres_fm_pl_gelu_kernel(
             for r in range(PACK):
                 xr_pass(a, h, r, 0, HALF, False)
 
-        def close(h):
-            for lo, hi in ((0, QUARTER), (QUARTER, LAST), (LAST, HALF)):
-                xr_pass(PASSES - 1, h, 0, lo, hi, hi == HALF)
-            for r in range(1, PACK):
-                xr_pass(PASSES - 1, h, r, 0, HALF, True)
+        def first_quarter(h):
+            for r in range(PACK):
+                xr_pass(PASSES - 1, h, r, 0, QUARTER, False)
+
+        def close(h, r):
+            if r == 0:
+                xr_pass(PASSES - 1, h, 0, QUARTER, LAST, False)
+                xr_pass(PASSES - 1, h, 0, LAST, HALF, True)
+            else:
+                xr_pass(PASSES - 1, h, r, QUARTER, HALF, True)
 
         def activate(h, r, lo, hi):
             nc.scalar.activation(
@@ -197,39 +203,56 @@ def tile_mix_xres_fm_pl_gelu_kernel(
                     in_=bias_row[:].rearrange("p (i r) -> p r i", r=PACK),
                 )
                 nc.vector.transpose(out=bias[:], in_=bias_dealt[:])
-        group(act, (2, 0), 0, 160)
-        group(vec, (2, 0), 160, HALF)
-        group(act, (2, 1), 0, QUARTER)
-        group(vec, (2, 1), QUARTER, LAST)
-        quantize((2, 0))
-        group(vec, (2, 1), LAST, HALF)
-        quantize((2, 1), 0, QUARTER)
-        quantize((2, 1), QUARTER, HALF)
+        for lo in (0, QUARTER):
+            group(act, (2, 0), lo + 160, lo + QUARTER)
+            group(vec, (2, 0), lo, lo + 160)
+        quantize((2, 0), 0, QUARTER)
+        group(vec, (2, 1), 0, 96)
+        quantize((2, 0), QUARTER, HALF)
+        group(act, (2, 1), 192, 352)
         multiply_x4(3, 0)
-        multiply_xr(2, 0)
-        multiply_xr(2, 1)
-        group(act, (3, 0), HALF - 192, HALF)
-        group(vec, (3, 0), 0, QUARTER)
-        group(vec, (3, 0), QUARTER, HALF - 192)
+        for lo in (0, QUARTER):
+            for r in range(PACK):
+                xr_pass(2, 0, r, lo, lo + QUARTER, False)
+        group(act, (3, 0), 160, QUARTER)
+        group(vec, (3, 0), 0, 160)
+        group(vec, (2, 1), 96, 192)
         quantize((3, 0), 0, QUARTER)
+        quantize((2, 1), 0, QUARTER)
+        group(act, (2, 1), 352, HALF)
+        first_quarter(0)
+        for r in range(PACK - 1):
+            xr_pass(2, 1, r, 0, QUARTER, False)
+        group(act, (3, 0), LAST, HALF)
+        group(vec, (3, 0), QUARTER, LAST)
+        quantize((2, 1), QUARTER, HALF)
         quantize((3, 0), QUARTER, LAST)
         quantize((3, 0), LAST, HALF)
-        close(0)
+        for r in range(PACK):
+            close(0, r)
         for r in range(PACK - 1):
             activate(0, r, 0, HALF)
         activate(0, PACK - 1, 0, QUARTER)
         activate(0, PACK - 1, QUARTER, HALF)
-        group(vec, (3, 1), 0, QUARTER)
-        group(vec, (3, 1), QUARTER, HALF)
-        quantize((3, 1), 0, QUARTER)
+        xr_pass(2, 1, PACK - 1, 0, QUARTER, False)
+        for r in range(PACK):
+            xr_pass(2, 1, r, QUARTER, HALF, False)
+        group(vec, (3, 1), 0, 128)
+        group(vec, (3, 1), 128, QUARTER)
+        quantize((3, 1), 0, 128)
+        quantize((3, 1), 128, QUARTER)
+        first_quarter(1)
+        group(vec, (3, 1), QUARTER, LAST)
+        group(vec, (3, 1), LAST, HALF)
         quantize((3, 1), QUARTER, LAST)
         quantize((3, 1), LAST, HALF)
         round_result(vec, 0, 0, QUARTER)
         round_result(vec, 0, QUARTER, HALF)
         quantize_result(0, 0, QUARTER)
         quantize_result(0, QUARTER, HALF)
-        multiply_x4(3, 1)
-        close(1)
+        for r in range(PACK):
+            multiply_x4(3, 1, (r,))
+            close(1, r)
         activate(1, 0, 0, HALF)
         activate(1, 1, 0, HALF)
         for lo, hi in ((0, QUARTER), (QUARTER, LAST), (LAST, HALF)):

@@ -23,6 +23,7 @@ QUARTER = 256
 SCALAR_COLS = 224
 LAST = 384
 ALIGN = 256
+LAST_LOADS = ((0, HALF), (HALF, HALF + QUARTER), (HALF + QUARTER, T))
 
 
 def interleave(copy, dst, src):
@@ -94,10 +95,10 @@ def tile_mix_xres_fm_pl_gelu_kernel(
             if a == 0:
                 nc.sync.dma_start(out=bias_row[0:P:32, :], in_=b.rearrange("(q n) -> q n", n=P))
         nc.sync.dma_start(out=x4_last[0][:].bitcast(I32), in_=x4_rows[:, 3, :QUARTER])
-        raw_last = []
-        for c in range(T // QUARTER):
-            raw_last.append(tile([P, PACK, QUARTER], F32, f"raw_last{c}"))
-            nc.sync.dma_start(out=raw_last[c][:], in_=xr_rows[PASSES - 1][:, :, c * QUARTER : (c + 1) * QUARTER])
+        raw_last = {}
+        for lo, hi in LAST_LOADS:
+            raw_last[lo, hi] = tile([P, PACK, hi - lo], F32, f"raw_last{lo}")
+            nc.sync.dma_start(out=raw_last[lo, hi][:], in_=xr_rows[PASSES - 1][:, :, lo:hi])
         nc.sync.dma_start(out=x4_last[1][:].bitcast(I32), in_=x4_rows[:, 3, QUARTER:])
 
         for a in range(PASSES):
@@ -112,10 +113,12 @@ def tile_mix_xres_fm_pl_gelu_kernel(
 
         def group(copy, piece, lo, hi):
             a, h = piece
+            first, last = h * HALF + lo, h * HALF + hi
             if a < PASSES - 1:
-                src = raw[a][:, :, h * HALF + lo : h * HALF + hi]
+                src = raw[a][:, :, first:last]
             else:
-                src = raw_last[2 * h + lo // QUARTER][:, :, lo % QUARTER : (hi - 1) % QUARTER + 1]
+                key = [k for k in LAST_LOADS if k[0] <= first and last <= k[1]][0]
+                src = raw_last[key][:, :, first - key[0] : last - key[0]]
             interleave(copy, grouped[piece][:, lo:hi, :], src)
 
         def group_shared(piece):
@@ -206,35 +209,32 @@ def tile_mix_xres_fm_pl_gelu_kernel(
         for lo in (0, QUARTER):
             group(act, (2, 0), lo + 160, lo + QUARTER)
             group(vec, (2, 0), lo, lo + 160)
+        group(act, (2, 1), 0, 240)
         quantize((2, 0), 0, QUARTER)
-        group(vec, (2, 1), 0, 96)
+        group(vec, (2, 1), 240, 384)
         quantize((2, 0), QUARTER, HALF)
-        group(act, (2, 1), 192, 352)
-        multiply_x4(3, 0)
-        for lo in (0, QUARTER):
-            for r in range(PACK):
-                xr_pass(2, 0, r, lo, lo + QUARTER, False)
-        group(act, (3, 0), 160, QUARTER)
-        group(vec, (3, 0), 0, 160)
-        group(vec, (2, 1), 96, 192)
-        quantize((3, 0), 0, QUARTER)
+        group(vec, (2, 1), 384, HALF)
         quantize((2, 1), 0, QUARTER)
-        group(act, (2, 1), 352, HALF)
-        first_quarter(0)
-        for r in range(PACK - 1):
-            xr_pass(2, 1, r, 0, QUARTER, False)
+        multiply_x4(3, 0)
+        for h, lo in ((0, 0), (0, QUARTER), (1, 0)):
+            for r in range(PACK):
+                xr_pass(2, h, r, lo, lo + QUARTER, False)
+        group(act, (3, 0), 288, LAST)
         group(act, (3, 0), LAST, HALF)
-        group(vec, (3, 0), QUARTER, LAST)
-        quantize((2, 1), QUARTER, HALF)
+        group(vec, (3, 0), 0, QUARTER)
+        group(vec, (3, 0), QUARTER, 288)
+        quantize((3, 0), 0, QUARTER)
         quantize((3, 0), QUARTER, LAST)
         quantize((3, 0), LAST, HALF)
-        for r in range(PACK):
-            close(0, r)
+        quantize((2, 1), QUARTER, HALF)
+        xr_pass(3, 0, 0, 0, QUARTER, False)
+        close(0, 0)
+        for r in range(1, PACK):
+            xr_pass(3, 0, r, 0, HALF, True)
         for r in range(PACK - 1):
             activate(0, r, 0, HALF)
         activate(0, PACK - 1, 0, QUARTER)
         activate(0, PACK - 1, QUARTER, HALF)
-        xr_pass(2, 1, PACK - 1, 0, QUARTER, False)
         for r in range(PACK):
             xr_pass(2, 1, r, QUARTER, HALF, False)
         group(vec, (3, 1), 0, 128)

@@ -33,6 +33,10 @@ def interleave(copy, dst, src):
     )
 
 
+def flat(rows):
+    return rows.rearrange("p j t -> p (j t)")
+
+
 def tile_mix_xres_fm_pl_gelu_kernel(
     tc, x4_words, x4_scales, xr, w4_words, w4_scales, b, out_0, out_1, out_2
 ):
@@ -91,10 +95,12 @@ def tile_mix_xres_fm_pl_gelu_kernel(
         raw = []
         for a in range(PASSES - 1):
             raw.append(tile([P, PACK, T], F32, f"raw{a}"))
-            nc.sync.dma_start(out=raw[a][:], in_=xr_rows[a])
+            run = PACK * T if a < PASSES - 2 else PACK * T - HALF
+            nc.sync.dma_start(out=flat(raw[a][:])[:, :run], in_=flat(xr_rows[a])[:, :run])
             if a == 0:
                 nc.sync.dma_start(out=bias_row[0:P:32, :], in_=b.rearrange("(q n) -> q n", n=P))
-        nc.sync.dma_start(out=x4_last[0][:].bitcast(I32), in_=x4_rows[:, 3, :QUARTER])
+                nc.sync.dma_start(out=x4_last[0][:].bitcast(I32), in_=x4_rows[:, 3, :QUARTER])
+        nc.sync.dma_start(out=raw[2][:, PACK - 1, HALF:], in_=xr_rows[2][:, PACK - 1, HALF:])
         raw_last = {}
         for lo, hi in LAST_LOADS:
             raw_last[lo, hi] = tile([P, PACK, hi - lo], F32, f"raw_last{lo}")
@@ -201,24 +207,27 @@ def tile_mix_xres_fm_pl_gelu_kernel(
             multiply_xr(a, 1)
             if a == 0:
                 multiply_x4(2, 1)
+                multiply_x4(3, 0)
                 nc.vector.tensor_copy(
                     out=bias_dealt[:].rearrange("p (r i) -> p r i", r=PACK),
                     in_=bias_row[:].rearrange("p (i r) -> p r i", r=PACK),
                 )
                 nc.vector.transpose(out=bias[:], in_=bias_dealt[:])
-        for lo in (0, QUARTER):
-            group(act, (2, 0), lo + 160, lo + QUARTER)
-            group(vec, (2, 0), lo, lo + 160)
-        group(act, (2, 1), 0, 240)
+        group(act, (2, 0), 304, HALF)
+        group(act, (2, 1), 0, 160)
+        group(act, (2, 1), QUARTER, 400)
+        group(vec, (2, 0), 0, QUARTER)
+        group(vec, (2, 0), QUARTER, 304)
         quantize((2, 0), 0, QUARTER)
-        group(vec, (2, 1), 240, 384)
+        group(vec, (2, 1), 160, QUARTER)
         quantize((2, 0), QUARTER, HALF)
-        group(vec, (2, 1), 384, HALF)
+        group(vec, (2, 1), 400, HALF)
         quantize((2, 1), 0, QUARTER)
-        multiply_x4(3, 0)
-        for h, lo in ((0, 0), (0, QUARTER), (1, 0)):
-            for r in range(PACK):
-                xr_pass(2, h, r, lo, lo + QUARTER, False)
+        quantize((2, 1), QUARTER, HALF)
+        for h in range(2):
+            for lo in (0, QUARTER):
+                for r in range(PACK):
+                    xr_pass(2, h, r, lo, lo + QUARTER, False)
         group(act, (3, 0), 288, LAST)
         group(act, (3, 0), LAST, HALF)
         group(vec, (3, 0), 0, QUARTER)
@@ -226,21 +235,17 @@ def tile_mix_xres_fm_pl_gelu_kernel(
         quantize((3, 0), 0, QUARTER)
         quantize((3, 0), QUARTER, LAST)
         quantize((3, 0), LAST, HALF)
-        quantize((2, 1), QUARTER, HALF)
         xr_pass(3, 0, 0, 0, QUARTER, False)
         close(0, 0)
         for r in range(1, PACK):
             xr_pass(3, 0, r, 0, HALF, True)
+        group(act, (3, 1), 128, QUARTER)
         for r in range(PACK - 1):
             activate(0, r, 0, HALF)
         activate(0, PACK - 1, 0, QUARTER)
         activate(0, PACK - 1, QUARTER, HALF)
-        for r in range(PACK):
-            xr_pass(2, 1, r, QUARTER, HALF, False)
         group(vec, (3, 1), 0, 128)
-        group(vec, (3, 1), 128, QUARTER)
-        quantize((3, 1), 0, 128)
-        quantize((3, 1), 128, QUARTER)
+        quantize((3, 1), 0, QUARTER)
         first_quarter(1)
         group(vec, (3, 1), QUARTER, LAST)
         group(vec, (3, 1), LAST, HALF)

@@ -23,7 +23,7 @@ QUARTER = 256
 SCALAR_COLS = 224
 LAST = 384
 ALIGN = 256
-LAST_LOADS = ((0, HALF), (HALF, HALF + QUARTER), (HALF + QUARTER, T))
+LAST_LOADS = ((0, 256), (256, 512), (512, 768), (768, 896), (896, 1024))
 
 
 def interleave(copy, dst, src):
@@ -165,10 +165,6 @@ def tile_mix_xres_fm_pl_gelu_kernel(
             for r in range(PACK):
                 xr_pass(a, h, r, 0, HALF, False)
 
-        def first_quarter(h):
-            for r in range(PACK):
-                xr_pass(PASSES - 1, h, r, 0, QUARTER, False)
-
         def close(h, r):
             if r == 0:
                 xr_pass(PASSES - 1, h, 0, QUARTER, LAST, False)
@@ -213,40 +209,45 @@ def tile_mix_xres_fm_pl_gelu_kernel(
                     in_=bias_row[:].rearrange("p (i r) -> p r i", r=PACK),
                 )
                 nc.vector.transpose(out=bias[:], in_=bias_dealt[:])
-        group(act, (2, 0), 304, HALF)
-        group(act, (2, 1), 0, 160)
-        group(act, (2, 1), QUARTER, 400)
-        group(vec, (2, 0), 0, QUARTER)
-        group(vec, (2, 0), QUARTER, 304)
-        quantize((2, 0), 0, QUARTER)
-        group(vec, (2, 1), 160, QUARTER)
-        quantize((2, 0), QUARTER, HALF)
-        group(vec, (2, 1), 400, HALF)
+        def multiply_quarter(a, h, lo, rows=range(PACK)):
+            for r in rows:
+                xr_pass(a, h, r, lo, lo + QUARTER, False)
+
+        for lo in (0, QUARTER):
+            group(act, (2, 0), lo + 160, lo + QUARTER)
+            group(vec, (2, 0), lo, lo + 160)
+        group(act, (2, 1), 0, 144)
+        for lo in (0, QUARTER):
+            quantize((2, 0), lo, lo + QUARTER)
+            multiply_quarter(2, 0, lo)
+        group(vec, (2, 1), 144, QUARTER)
+        group(act, (3, 0), 160, QUARTER)
+        group(vec, (3, 0), 0, 160)
         quantize((2, 1), 0, QUARTER)
-        quantize((2, 1), QUARTER, HALF)
-        for h in range(2):
-            for lo in (0, QUARTER):
-                for r in range(PACK):
-                    xr_pass(2, h, r, lo, lo + QUARTER, False)
-        group(act, (3, 0), 288, LAST)
-        group(act, (3, 0), LAST, HALF)
-        group(vec, (3, 0), 0, QUARTER)
-        group(vec, (3, 0), QUARTER, 288)
         quantize((3, 0), 0, QUARTER)
+        group(act, (2, 1), QUARTER, 368)
+        group(vec, (2, 1), 448, HALF)
+        multiply_quarter(2, 1, 0)
+        multiply_quarter(3, 0, 0)
+        group(act, (3, 0), QUARTER + 160, HALF)
+        group(vec, (3, 0), QUARTER, LAST)
+        group(vec, (3, 0), LAST, QUARTER + 160)
         quantize((3, 0), QUARTER, LAST)
         quantize((3, 0), LAST, HALF)
-        xr_pass(3, 0, 0, 0, QUARTER, False)
-        close(0, 0)
-        for r in range(1, PACK):
-            xr_pass(3, 0, r, 0, HALF, True)
-        group(act, (3, 1), 128, QUARTER)
+        group(act, (2, 1), 368, 448)
+        quantize((2, 1), QUARTER, HALF)
+        for r in range(PACK):
+            close(0, r)
         for r in range(PACK - 1):
             activate(0, r, 0, HALF)
         activate(0, PACK - 1, 0, QUARTER)
         activate(0, PACK - 1, QUARTER, HALF)
         group(vec, (3, 1), 0, 128)
-        quantize((3, 1), 0, QUARTER)
-        first_quarter(1)
+        group(vec, (3, 1), 128, QUARTER)
+        quantize((3, 1), 0, 128)
+        quantize((3, 1), 128, QUARTER)
+        multiply_quarter(2, 1, QUARTER)
+        multiply_quarter(3, 1, 0)
         group(vec, (3, 1), QUARTER, LAST)
         group(vec, (3, 1), LAST, HALF)
         quantize((3, 1), QUARTER, LAST)

@@ -23,7 +23,7 @@ QUARTER = 256
 SCALAR_COLS = 224
 LAST = 384
 ALIGN = 256
-LAST_LOADS = ((0, 256), (256, 512), (512, 768), (768, 896), (896, 1024))
+LAST_LOADS = ((0, 256), (256, 384), (384, 512), (512, 640), (640, 768), (768, 896), (896, 960), (960, 1024))
 
 
 def interleave(copy, dst, src):
@@ -216,42 +216,43 @@ def tile_mix_xres_fm_pl_gelu_kernel(
         for lo in (0, QUARTER):
             group(act, (2, 0), lo + 160, lo + QUARTER)
             group(vec, (2, 0), lo, lo + 160)
-        group(act, (2, 1), 0, 144)
+        group(act, (2, 1), 0, 192)
         for lo in (0, QUARTER):
             quantize((2, 0), lo, lo + QUARTER)
             multiply_quarter(2, 0, lo)
-        group(vec, (2, 1), 144, QUARTER)
+        group(vec, (2, 1), 192, 352)
         group(act, (3, 0), 160, QUARTER)
         group(vec, (3, 0), 0, 160)
         quantize((2, 1), 0, QUARTER)
         quantize((3, 0), 0, QUARTER)
-        group(act, (2, 1), QUARTER, 368)
-        group(vec, (2, 1), 448, HALF)
-        multiply_quarter(2, 1, 0)
+        group(act, (2, 1), 352, HALF)
+        multiply_quarter(2, 1, 0, range(PACK - 1))
         multiply_quarter(3, 0, 0)
-        group(act, (3, 0), QUARTER + 160, HALF)
         group(vec, (3, 0), QUARTER, LAST)
-        group(vec, (3, 0), LAST, QUARTER + 160)
+        group(act, (3, 0), 448, HALF)
+        group(vec, (3, 0), LAST, 448)
         quantize((3, 0), QUARTER, LAST)
         quantize((3, 0), LAST, HALF)
-        group(act, (2, 1), 368, 448)
         quantize((2, 1), QUARTER, HALF)
+        group(act, (3, 1), 0, 128)
         for r in range(PACK):
             close(0, r)
         for r in range(PACK - 1):
             activate(0, r, 0, HALF)
         activate(0, PACK - 1, 0, QUARTER)
         activate(0, PACK - 1, QUARTER, HALF)
-        group(vec, (3, 1), 0, 128)
         group(vec, (3, 1), 128, QUARTER)
         quantize((3, 1), 0, 128)
+        group(vec, (3, 1), QUARTER, LAST)
         quantize((3, 1), 128, QUARTER)
+        multiply_quarter(2, 1, 0, (PACK - 1,))
         multiply_quarter(2, 1, QUARTER)
         multiply_quarter(3, 1, 0)
-        group(vec, (3, 1), QUARTER, LAST)
-        group(vec, (3, 1), LAST, HALF)
+        group(vec, (3, 1), LAST, 448)
         quantize((3, 1), QUARTER, LAST)
-        quantize((3, 1), LAST, HALF)
+        group(vec, (3, 1), 448, HALF)
+        quantize((3, 1), LAST, 448)
+        quantize((3, 1), 448, HALF)
         round_result(vec, 0, 0, QUARTER)
         round_result(vec, 0, QUARTER, HALF)
         quantize_result(0, 0, QUARTER)

@@ -23,7 +23,7 @@ QUARTER = 256
 SCALAR_COLS = 224
 LAST = 384
 ALIGN = 256
-LAST_LOADS = ((0, 256), (256, 384), (384, 512), (512, 640), (640, 768), (768, 896), (896, 960), (960, 1024))
+LAST_LOADS = ((0, 256), (256, 384), (384, 512), (512, 640), (640, 768), (768, 896), (896, 1024))
 
 
 def interleave(copy, dst, src):
@@ -33,8 +33,8 @@ def interleave(copy, dst, src):
     )
 
 
-def flat(rows):
-    return rows.rearrange("p j t -> p (j t)")
+def row_pairs(rows):
+    return rows.rearrange("p (u j) t -> p u (j t)", u=2)
 
 
 def tile_mix_xres_fm_pl_gelu_kernel(
@@ -53,8 +53,9 @@ def tile_mix_xres_fm_pl_gelu_kernel(
         ws_raw = tile([P, PASSES, M], U8, "ws_raw")
         w_codes = [tile([P, 2 * M], U8, f"w_codes{a}") for a in range(PASSES)]
         w_planes = [tile([P, M], U8, f"w_planes{a}") for a in range(PASSES)]
-        x4_codes = tile([P, PASSES - 1, 2 * T], U8, "x4_codes")
-        x4_last = [tile([P, 2 * HALF], U8, f"x4_last{h}") for h in range(2)]
+        x4_left = tile([P, PASSES, 2 * HALF], U8, "x4_left")
+        x4_right = tile([P, PASSES - 1, 2 * HALF], U8, "x4_right")
+        x4_last = tile([P, 2 * HALF], U8, "x4_last")
         x4_planes = tile([P, PASSES, T], U8, "x4_planes")
         bias_row = tile([P, P], F32, "bias_row")
         bias_dealt = tile([P, P], F32, "bias_dealt")
@@ -89,23 +90,23 @@ def tile_mix_xres_fm_pl_gelu_kernel(
 
         nc.sync.dma_start(out=w_raw[:].bitcast(I32), in_=w_rows)
         load_planes(ws_raw, w4_scales)
-        nc.sync.dma_start(out=x4_codes[:, :2, :].bitcast(I32), in_=x4_rows[:, :2, :])
+        nc.sync.dma_start(out=x4_left[:].bitcast(I32), in_=x4_rows[:, :, :QUARTER])
         load_planes(x4_planes, x4_scales)
-        nc.sync.dma_start(out=x4_codes[:, 2:3, :].bitcast(I32), in_=x4_rows[:, 2:3, :])
+        nc.sync.dma_start(out=x4_right[:].bitcast(I32), in_=x4_rows[:, : PASSES - 1, QUARTER:])
         raw = []
         for a in range(PASSES - 1):
             raw.append(tile([P, PACK, T], F32, f"raw{a}"))
-            run = PACK * T if a < PASSES - 2 else PACK * T - HALF
-            nc.sync.dma_start(out=flat(raw[a][:])[:, :run], in_=flat(xr_rows[a])[:, :run])
+            if a < PASSES - 2:
+                nc.sync.dma_start(out=raw[a][:], in_=xr_rows[a])
             if a == 0:
                 nc.sync.dma_start(out=bias_row[0:P:32, :], in_=b.rearrange("(q n) -> q n", n=P))
-                nc.sync.dma_start(out=x4_last[0][:].bitcast(I32), in_=x4_rows[:, 3, :QUARTER])
-        nc.sync.dma_start(out=raw[2][:, PACK - 1, HALF:], in_=xr_rows[2][:, PACK - 1, HALF:])
+        for run in (slice(0, T + HALF), slice(T + HALF, 2 * T)):
+            nc.sync.dma_start(out=row_pairs(raw[2][:])[:, :, run], in_=row_pairs(xr_rows[2])[:, :, run])
         raw_last = {}
         for lo, hi in LAST_LOADS:
             raw_last[lo, hi] = tile([P, PACK, hi - lo], F32, f"raw_last{lo}")
             nc.sync.dma_start(out=raw_last[lo, hi][:], in_=xr_rows[PASSES - 1][:, :, lo:hi])
-        nc.sync.dma_start(out=x4_last[1][:].bitcast(I32), in_=x4_rows[:, 3, QUARTER:])
+        nc.sync.dma_start(out=x4_last[:].bitcast(I32), in_=x4_rows[:, PASSES - 1, QUARTER:])
 
         for a in range(PASSES):
             nc.vector.tensor_copy(
@@ -150,7 +151,7 @@ def tile_mix_xres_fm_pl_gelu_kernel(
             )
 
         def multiply_x4(a, h, rows=range(PACK)):
-            codes = x4_last[h][:] if a == PASSES - 1 else x4_codes[:, a, 2 * HALF * h : 2 * HALF * (h + 1)]
+            codes = x4_left[:, a, :] if h == 0 else x4_right[:, a, :] if a < PASSES - 1 else x4_last[:]
             for r in rows:
                 one_pass(
                     acc[h, r][:], a, r, codes.bitcast(FP4X4), x4_planes[:, a, HALF * h : HALF * (h + 1)], a == 0, False
@@ -189,11 +190,9 @@ def tile_mix_xres_fm_pl_gelu_kernel(
             )
 
         vec, act = nc.vector.tensor_copy, nc.scalar.copy
-        multiply_x4(0, 0)
+        for a in range(PASSES):
+            multiply_x4(a, 0)
         multiply_x4(0, 1)
-        multiply_x4(1, 0)
-        multiply_x4(1, 1)
-        multiply_x4(2, 0)
         for a in range(PASSES - 2):
             group_shared((a, 0))
             group_shared((a, 1))
@@ -202,8 +201,8 @@ def tile_mix_xres_fm_pl_gelu_kernel(
             multiply_xr(a, 0)
             multiply_xr(a, 1)
             if a == 0:
+                multiply_x4(1, 1)
                 multiply_x4(2, 1)
-                multiply_x4(3, 0)
                 nc.vector.tensor_copy(
                     out=bias_dealt[:].rearrange("p (r i) -> p r i", r=PACK),
                     in_=bias_row[:].rearrange("p (i r) -> p r i", r=PACK),
@@ -216,25 +215,27 @@ def tile_mix_xres_fm_pl_gelu_kernel(
         for lo in (0, QUARTER):
             group(act, (2, 0), lo + 160, lo + QUARTER)
             group(vec, (2, 0), lo, lo + 160)
-        group(act, (2, 1), 0, 192)
         for lo in (0, QUARTER):
             quantize((2, 0), lo, lo + QUARTER)
             multiply_quarter(2, 0, lo)
-        group(vec, (2, 1), 192, 352)
+        for lo in (0, QUARTER):
+            group(act, (2, 1), lo, lo + 128)
+            group(vec, (2, 1), lo + 128, lo + QUARTER)
+        quantize((2, 1), 0, QUARTER)
+        multiply_quarter(2, 1, 0)
         group(act, (3, 0), 160, QUARTER)
         group(vec, (3, 0), 0, 160)
-        quantize((2, 1), 0, QUARTER)
+        quantize((2, 1), QUARTER, HALF)
         quantize((3, 0), 0, QUARTER)
-        group(act, (2, 1), 352, HALF)
-        multiply_quarter(2, 1, 0, range(PACK - 1))
+        multiply_quarter(2, 1, QUARTER, range(2))
         multiply_quarter(3, 0, 0)
-        group(vec, (3, 0), QUARTER, LAST)
+        group(act, (3, 0), QUARTER, LAST)
         group(act, (3, 0), 448, HALF)
         group(vec, (3, 0), LAST, 448)
         quantize((3, 0), QUARTER, LAST)
         quantize((3, 0), LAST, HALF)
-        quantize((2, 1), QUARTER, HALF)
-        group(act, (3, 1), 0, 128)
+        group(act, (3, 1), 64, 128)
+        group(vec, (3, 1), 0, 64)
         for r in range(PACK):
             close(0, r)
         for r in range(PACK - 1):
@@ -243,16 +244,13 @@ def tile_mix_xres_fm_pl_gelu_kernel(
         activate(0, PACK - 1, QUARTER, HALF)
         group(vec, (3, 1), 128, QUARTER)
         quantize((3, 1), 0, 128)
-        group(vec, (3, 1), QUARTER, LAST)
         quantize((3, 1), 128, QUARTER)
-        multiply_quarter(2, 1, 0, (PACK - 1,))
-        multiply_quarter(2, 1, QUARTER)
+        group(vec, (3, 1), QUARTER, LAST)
+        multiply_quarter(2, 1, QUARTER, range(2, PACK))
         multiply_quarter(3, 1, 0)
-        group(vec, (3, 1), LAST, 448)
+        group(vec, (3, 1), LAST, HALF)
         quantize((3, 1), QUARTER, LAST)
-        group(vec, (3, 1), 448, HALF)
-        quantize((3, 1), LAST, 448)
-        quantize((3, 1), 448, HALF)
+        quantize((3, 1), LAST, HALF)
         round_result(vec, 0, 0, QUARTER)
         round_result(vec, 0, QUARTER, HALF)
         quantize_result(0, 0, QUARTER)

from contextlib import ExitStack

import concourse.mybir as mybir

K, M, T = 2048, 512, 1024
FLOPS = 2 * 2 * K * M * T

F32 = mybir.dt.float32
BF16 = mybir.dt.bfloat16
I32 = mybir.dt.int32
U32 = mybir.dt.uint32
U16 = mybir.dt.uint16
U8 = mybir.dt.uint8
FP8X4 = mybir.dt.float8_e4m3fn_x4
FP4X4 = mybir.dt.float4_e2m1fn_x4
GELU = mybir.ActivationFunctionType.Gelu_apprx_tanh

P = 128
PACK = 4
PASSES = K // (P * PACK)
HALF = 512
QUARTER = 256
SCALAR_COLS = 224
LAST = 384
ALIGN = 256
LAST_LOADS = ((0, 256), (256, 384), (384, 512), (512, 640), (640, 768), (768, 896), (896, 1024))


def interleave(copy, dst, src):
    copy(
        out=dst.rearrange("p (c i) j -> p c j i", i=8),
        in_=src.rearrange("p j (c i) -> p c j i", i=8),
    )


def row_pairs(rows):
    return rows.rearrange("p (u j) t -> p u (j t)", u=2)


def tile_mix_xres_fm_pl_gelu_kernel(
    tc, x4_words, x4_scales, xr, w4_words, w4_scales, b, out_0, out_1, out_2
):
    nc = tc.nc
    with ExitStack() as ctx:
        sb = ctx.enter_context(tc.tile_pool(name="sb", bufs=1))
        ps = ctx.enter_context(tc.psum_pool(name="ps", bufs=1))
        ctx.enter_context(tc.manual_schedule())

        def tile(shape, dtype, name):
            return sb.tile(shape, dtype, align_bytes=ALIGN, name=name)

        w_raw = tile([P, PASSES, 2 * M], U8, "w_raw")
        ws_raw = tile([P, PASSES, M], U8, "ws_raw")
        w_codes = [tile([P, 2 * M], U8, f"w_codes{a}") for a in range(PASSES)]
        w_planes = [tile([P, M], U8, f"w_planes{a}") for a in range(PASSES)]
        x4_left = tile([P, PASSES, 2 * HALF], U8, "x4_left")
        x4_right = tile([P, PASSES - 1, 2 * HALF], U8, "x4_right")
        x4_last = tile([P, 2 * HALF], U8, "x4_last")
        x4_planes = tile([P, PASSES, T], U8, "x4_planes")
        bias_row = tile([P, P], F32, "bias_row")
        bias_dealt = tile([P, P], F32, "bias_dealt")
        bias = tile([P, P], F32, "bias")
        pieces = [(a, h) for a in range(PASSES) for h in range(2)]
        grouped = {k: tile([P, HALF, PACK], BF16, f"grouped{k[0]}{k[1]}") for k in pieces}
        xr_codes = {k: tile([P, HALF], U32, f"xr_codes{k[0]}{k[1]}") for k in pieces}
        xr_scales = {k: tile([P, HALF], U8, f"xr_scales{k[0]}{k[1]}") for k in pieces}
        acc = {(h, r): ps.tile([P, HALF], F32, name=f"acc{h}{r}") for h in range(2) for r in range(PACK)}
        result = [tile([P, PACK, HALF], F32, f"result{h}") for h in range(2)]
        rounded = [tile([P, HALF, PACK], BF16, f"rounded{h}") for h in range(2)]
        out_codes = tile([P, T], U32, "out_codes")
        out_scales = tile([P, T], U8, "out_scales")

        warm = tile([P, 8], F32, "warm")
        nc.gpsimd.memset(warm[:], 0.0)
        nc.scalar.activation(out=warm[:, 4:5], in_=warm[:, 0:1], func=GELU)
        nc.vector.memset(ws_raw[:].bitcast(I32), 0)
        nc.vector.memset(x4_planes[:].bitcast(I32), 0)
        nc.vector.memset(bias_row[:], 0.0)

        w_rows = w4_words.rearrange("a p n -> p a n").bitcast(I32)
        x4_rows = x4_words.rearrange("a p n -> p a n").bitcast(I32)
        xr_rows = xr.rearrange("(a p j) t -> a p j t", p=P, j=PACK)

        def load_planes(plane, scales):
            for r in range(4):
                nc.sync.dma_start(
                    out=plane[r:P:32].bitcast(I32),
                    in_=scales.rearrange("a (q r) n -> r q a n", r=4)[r].bitcast(I32),
                )

        nc.sync.dma_start(out=w_raw[:].bitcast(I32), in_=w_rows)
        load_planes(ws_raw, w4_scales)
        nc.sync.dma_start(out=x4_left[:].bitcast(I32), in_=x4_rows[:, :, :QUARTER])
        load_planes(x4_planes, x4_scales)
        nc.sync.dma_start(out=x4_right[:].bitcast(I32), in_=x4_rows[:, : PASSES - 1, QUARTER:])
        raw = []
        for a in range(PASSES - 1):
            raw.append(tile([P, PACK, T], F32, f"raw{a}"))
            if a < PASSES - 2:
                nc.sync.dma_start(out=raw[a][:], in_=xr_rows[a])
            if a == 0:
                nc.sync.dma_start(out=bias_row[0:P:32, :], in_=b.rearrange("(q n) -> q n", n=P))
        for run in (slice(0, T + HALF), slice(T + HALF, 2 * T)):
            nc.sync.dma_start(out=row_pairs(raw[2][:])[:, :, run], in_=row_pairs(xr_rows[2])[:, :, run])
        raw_last = {}
        for lo, hi in LAST_LOADS:
            raw_last[lo, hi] = tile([P, PACK, hi - lo], F32, f"raw_last{lo}")
            nc.sync.dma_start(out=raw_last[lo, hi][:], in_=xr_rows[PASSES - 1][:, :, lo:hi])
        nc.sync.dma_start(out=x4_last[:].bitcast(I32), in_=x4_rows[:, PASSES - 1, QUARTER:])

        for a in range(PASSES):
            nc.vector.tensor_copy(
                out=w_codes[a][:].bitcast(U16).rearrange("p (r m) -> p r m", r=PACK),
                in_=w_raw[:, a, :].bitcast(U16).rearrange("p (m r) -> p r m", r=PACK),
            )
            nc.vector.tensor_copy(
                out=w_planes[a][:].rearrange("p (r m) -> p r m", r=PACK),
                in_=ws_raw[:, a, :].rearrange("p (m r) -> p r m", r=PACK),
            )

        def group(copy, piece, lo, hi):
            a, h = piece
            first, last = h * HALF + lo, h * HALF + hi
            if a < PASSES - 1:
                src = raw[a][:, :, first:last]
            else:
                key = [k for k in LAST_LOADS if k[0] <= first and last <= k[1]][0]
                src = raw_last[key][:, :, first - key[0] : last - key[0]]
            interleave(copy, grouped[piece][:, lo:hi, :], src)

        def group_shared(piece):
            group(nc.scalar.copy, piece, 0, SCALAR_COLS)
            group(nc.vector.tensor_copy, piece, SCALAR_COLS, HALF)

        def quantize(piece, lo=0, hi=HALF):
            nc.vector.quantize_mx(
                out=xr_codes[piece][:, lo:hi].bitcast(FP8X4),
                scales=xr_scales[piece][:, lo:hi],
                in_=grouped[piece][:, lo:hi, :].rearrange("p t j -> p (t j)"),
            )

        def one_pass(out, a, r, rhs, rhs_scale, start, stop):
            nc.tensor.matmul_mx(
                out=out,
                lhsT=w_codes[a][:, 2 * P * r : 2 * P * (r + 1)].bitcast(FP4X4),
                lhsT_scale=w_planes[a][:, P * r : P * (r + 1)],
                rhs=rhs,
                rhs_scale=rhs_scale,
                start=start,
                stop=stop,
            )

        def multiply_x4(a, h, rows=range(PACK)):
            codes = x4_left[:, a, :] if h == 0 else x4_right[:, a, :] if a < PASSES - 1 else x4_last[:]
            for r in rows:
                one_pass(
                    acc[h, r][:], a, r, codes.bitcast(FP4X4), x4_planes[:, a, HALF * h : HALF * (h + 1)], a == 0, False
                )

        def xr_pass(a, h, r, lo, hi, stop):
            one_pass(
                acc[h, r][:, lo:hi], a, r, xr_codes[a, h][:, lo:hi].bitcast(FP8X4), xr_scales[a, h][:, lo:hi], False, stop
            )

        def multiply_xr(a, h):
            for r in range(PACK):
                xr_pass(a, h, r, 0, HALF, False)

        def close(h, r):
            if r == 0:
                xr_pass(PASSES - 1, h, 0, QUARTER, LAST, False)
                xr_pass(PASSES - 1, h, 0, LAST, HALF, True)
            else:
                xr_pass(PASSES - 1, h, r, QUARTER, HALF, True)

        def activate(h, r, lo, hi):
            nc.scalar.activation(
                out=result[h][:, r, lo:hi], in_=acc[h, r][:, lo:hi], func=GELU, bias=bias[:, 32 * r : 32 * r + 1]
            )

        def round_result(copy, h, lo, hi):
            interleave(copy, rounded[h][:, lo:hi, :], result[h][:, :, lo:hi])

        def quantize_result(h, lo, hi):
            cols = slice(h * HALF + lo, h * HALF + hi)
            nc.vector.quantize_mx(
                out=out_codes[:, cols].bitcast(FP8X4),
                scales=out_scales[:, cols],
                in_=rounded[h][:, lo:hi, :].rearrange("p t j -> p (t j)"),
            )

        vec, act = nc.vector.tensor_copy, nc.scalar.copy
        for a in range(PASSES):
            multiply_x4(a, 0)
        multiply_x4(0, 1)
        for a in range(PASSES - 2):
            group_shared((a, 0))
            group_shared((a, 1))
            quantize((a, 0))
            quantize((a, 1))
            multiply_xr(a, 0)
            multiply_xr(a, 1)
            if a == 0:
                multiply_x4(1, 1)
                multiply_x4(2, 1)
                nc.vector.tensor_copy(
                    out=bias_dealt[:].rearrange("p (r i) -> p r i", r=PACK),
                    in_=bias_row[:].rearrange("p (i r) -> p r i", r=PACK),
                )
                nc.vector.transpose(out=bias[:], in_=bias_dealt[:])
        def multiply_quarter(a, h, lo, rows=range(PACK)):
            for r in rows:
                xr_pass(a, h, r, lo, lo + QUARTER, False)

        for lo in (0, QUARTER):
            group(act, (2, 0), lo + 160, lo + QUARTER)
            group(vec, (2, 0), lo, lo + 160)
        for lo in (0, QUARTER):
            quantize((2, 0), lo, lo + QUARTER)
            multiply_quarter(2, 0, lo)
        for lo in (0, QUARTER):
            group(act, (2, 1), lo, lo + 128)
            group(vec, (2, 1), lo + 128, lo + QUARTER)
        quantize((2, 1), 0, QUARTER)
        multiply_quarter(2, 1, 0)
        group(act, (3, 0), 160, QUARTER)
        group(vec, (3, 0), 0, 160)
        quantize((2, 1), QUARTER, HALF)
        quantize((3, 0), 0, QUARTER)
        multiply_quarter(2, 1, QUARTER, range(2))
        multiply_quarter(3, 0, 0)
        group(act, (3, 0), QUARTER, LAST)
        group(act, (3, 0), 448, HALF)
        group(vec, (3, 0), LAST, 448)
        quantize((3, 0), QUARTER, LAST)
        quantize((3, 0), LAST, HALF)
        group(act, (3, 1), 64, 128)
        group(vec, (3, 1), 0, 64)
        for r in range(PACK):
            close(0, r)
        for r in range(PACK - 1):
            activate(0, r, 0, HALF)
        activate(0, PACK - 1, 0, QUARTER)
        activate(0, PACK - 1, QUARTER, HALF)
        group(vec, (3, 1), 128, QUARTER)
        quantize((3, 1), 0, 128)
        quantize((3, 1), 128, QUARTER)
        group(vec, (3, 1), QUARTER, LAST)
        multiply_quarter(2, 1, QUARTER, range(2, PACK))
        multiply_quarter(3, 1, 0)
        group(vec, (3, 1), LAST, HALF)
        quantize((3, 1), QUARTER, LAST)
        quantize((3, 1), LAST, HALF)
        round_result(vec, 0, 0, QUARTER)
        round_result(vec, 0, QUARTER, HALF)
        quantize_result(0, 0, QUARTER)
        quantize_result(0, QUARTER, HALF)
        for r in range(PACK):
            multiply_x4(3, 1, (r,))
            close(1, r)
        activate(1, 0, 0, HALF)
        activate(1, 1, 0, HALF)
        for lo, hi in ((0, QUARTER), (QUARTER, LAST), (LAST, HALF)):
            activate(1, 2, lo, hi)
            activate(1, 3, lo, hi)
        round_result(vec, 1, 0, QUARTER)
        round_result(vec, 1, QUARTER, LAST)
        round_result(act, 1, LAST, HALF)
        quantize_result(1, 0, QUARTER)
        quantize_result(1, QUARTER, LAST)
        quantize_result(1, LAST, HALF)

        rows = out_0.rearrange("(p r) t -> p r t", r=PACK)
        words = out_1[0].rearrange("p t i -> p (t i)").bitcast(I32)
        for r in range(PACK):
            nc.sync.dma_start(out=rows[:, r, :HALF], in_=result[0][:, r, :])
        for r in range(2):
            nc.sync.dma_start(out=rows[:, r, HALF:], in_=result[1][:, r, :])
        nc.sync.dma_start(out=words[:, :HALF], in_=out_codes[:, :HALF].bitcast(I32))
        nc.sync.dma_start(out=rows[:, 2:, HALF:], in_=result[1][:, 2:, :])
        for lo, hi in ((HALF, HALF + LAST), (HALF + LAST, T)):
            nc.sync.dma_start(out=words[:, lo:hi], in_=out_codes[:, lo:hi].bitcast(I32))
        for r in range(4):
            queue = nc.sync if r == 0 else nc.scalar
            queue.dma_start(
                out=out_2[0].rearrange("(q r) t -> r q t", r=4)[r].bitcast(I32),
                in_=out_scales[r:P:32, :].bitcast(I32),
            )
